import numpy as np
import ml_dtypes


def mxq(x, axis, fmt="e4m3"):
    dtype, down = {"e4m3": (ml_dtypes.float8_e4m3fn, 7), "e5m2": (ml_dtypes.float8_e5m2, 14)}[fmt]
    v = np.moveaxis(np.asarray(x, np.float32).astype(ml_dtypes.bfloat16).astype(np.float64), axis, -1)
    blocks = v.reshape(v.shape[:-1] + (-1, 32))
    amax = np.abs(blocks).max(-1, keepdims=True)
    byte = np.maximum(np.where(amax > 0, np.frexp(amax)[1] - 1 + 127, 0) - down, 1)
    scale = np.exp2(byte - 127.0)
    codes = (blocks / scale).astype(np.float32).astype(dtype).astype(np.float64)
    return np.moveaxis((codes * scale).reshape(v.shape), -1, axis)


WIDE = False


def mx_kscale(k):
    if not WIDE:
        return np.ones(k)
    levels = np.array([10, -10, 5, -5, 0])
    if k % 512:
        return np.exp2(np.random.permutation(np.resize(levels, k // 32))).repeat(32)
    a = np.empty((k // 512, 16))
    for p in range(k // 512):
        a[p, :8] = np.random.permutation(np.resize(levels, 8))
        for g in range(8):
            far = levels[np.abs(levels - a[p, g]) >= 10]
            a[p, g + 8] = far[np.random.randint(len(far))]
    return np.exp2(a.ravel()).repeat(32)


def f64(x):
    return np.asarray(x).astype(np.float64)


def striped(idx):
    return np.tile(idx.reshape(-1, 16).T, (8, 1)).astype(np.uint16)


def unstriped(offs):
    return offs[:16].T.reshape(-1).astype(np.int64)


def pack_weight(w):
    k, n = w.shape
    w = f64(np.asarray(w, np.float32).astype(ml_dtypes.bfloat16)).reshape(k // 32, 32, n)
    amax = np.abs(w).max(1)
    byte = np.clip(np.where(amax > 0, np.frexp(amax)[1] - 1 + 127 - 7, 1), 1, 254)
    scaled = (w * np.exp2(127.0 - byte)[:, None, :]).reshape(k, n).astype(np.float32)
    words = np.ascontiguousarray(scaled.reshape(k // 512, 128, 4, n).transpose(0, 1, 3, 2)).astype(ml_dtypes.float8_e4m3fn).view(np.uint8)
    return words, np.ascontiguousarray(byte.astype(np.uint8).reshape(k // 512, 16, n))


def unpack_weight(words, scales):
    g, p, n, _ = words.shape
    vals = np.ascontiguousarray(words).view(ml_dtypes.float8_e4m3fn).astype(np.float64) * np.repeat(np.exp2(scales.astype(np.float64) - 127.0), 8, axis=1)[..., None]
    return vals.transpose(0, 1, 3, 2).reshape(g * 512, n)


def planes(y):
    n, m = y.shape
    v = y.astype(np.float32).astype(ml_dtypes.bfloat16).astype(np.float64).reshape(n // 32, 32, m)
    top = np.abs(v).max(1)
    byte = np.clip(np.where(top > 0, np.frexp(top)[1] - 1 + 127 - 7, 1), 1, 254)
    codes = (v * np.exp2(127.0 - byte)[:, None, :]).reshape(n, m).astype(np.float32).astype(ml_dtypes.float8_e4m3fn).view(np.uint8)
    words = codes.reshape(n // 512, 128, 4, m).transpose(0, 1, 3, 2)
    return np.ascontiguousarray(words), np.ascontiguousarray(byte.astype(np.uint8).reshape(n // 512, 16, m))


K, T, S, H, N = 512, 1024, 512, 512, 512


def setup_inputs():
    n = np.random.standard_normal
    s = mx_kscale(K)[:, None]
    u = mx_kscale(H)
    packed_xT = pack_weight(n((K, T)) * s)
    return {
        "x_words": packed_xT[0],
        "x_scales": packed_xT[1],
        "w1": (n((K, H)) / np.sqrt(2 * K) / s * u).astype(np.float32),
        "w2": (n((K, H)) / np.sqrt(2 * K) / s * u).astype(np.float32),
        "w3": (n((H, N)) / np.sqrt(H) / u[:, None]).astype(np.float32),
        "w4": (n((K, N)) / np.sqrt(K) / s).astype(np.float32),
        "offs": striped(np.random.permutation(T)[:S]),
        "dst": striped(np.random.permutation(T)[:S]),
    }


def reference(x_words, x_scales, w1, w2, w3, w4, offs, dst):
    xq = unpack_weight(x_words, x_scales)[:, unstriped(offs)]
    x_dst = unpack_weight(x_words, x_scales)[:, unstriped(dst)]
    y = mxq(f64(w1), 0, "e4m3").T @ xq + mxq(f64(w2), 0, "e4m3").T @ x_dst
    h = np.maximum(y, 0.2 * y)
    e = np.exp(mxq(f64(w3), 0, "e4m3").T @ mxq(h, 0, "e4m3"))
    v = mxq(f64(w4), 0, "e4m3").T @ xq
    out_0 = e * v
    return (out_0,) + planes(out_0)

@@ -1,0 +1,212 @@
+from contextlib import ExitStack
+
+import concourse.mybir as mybir
+
+K, T, S, H, N = 512, 1024, 512, 512, 512
+FLOPS = 2 * S * (2 * K * H + H * N + K * N)
+
+F32 = mybir.dt.float32
+BF16 = mybir.dt.bfloat16
+I32 = mybir.dt.int32
+U32 = mybir.dt.uint32
+U16 = mybir.dt.uint16
+U8 = mybir.dt.uint8
+FP8X4 = mybir.dt.float8_e4m3fn_x4
+ALU = mybir.AluOpType
+ACT = mybir.ActivationFunctionType
+
+P = 128
+PACK = 4
+CHUNK = 128
+CHUNKS = S // CHUNK
+HALF = 256
+SLOPE = 0.2
+
+
+def tile_picked_zgatt_exp_po_kernel(
+    tc, x_words, x_scales, w1, w2, w3, w4, offs, dst, out_0, out_1, out_2
+):
+    nc = tc.nc
+    with ExitStack() as ctx:
+        keep = ctx.enter_context(tc.tile_pool(name="keep", bufs=1))
+        psum = ctx.enter_context(tc.psum_pool(name="psum", bufs=1))
+
+        table_words = keep.tile([P, T], I32, name="table_words")
+        table_scales = keep.tile([P, T], U8, name="table_scales")
+        src_list = keep.tile([P, S // 16], U16, name="src_list")
+        dst_list = keep.tile([P, S // 16], U16, name="dst_list")
+
+        nc.vector.memset(table_scales[:].bitcast(I32), 0)
+        warm = keep.tile([P, 2], F32, name="warm")
+        nc.vector.memset(warm[:, 0:1], 0.0)
+
+        nc.sync.dma_start(src_list[:], offs)
+        nc.sync.dma_start(dst_list[:], dst)
+        for q in range(4):
+            nc.scalar.dma_start(
+                table_scales[32 * q : 32 * q + 4, :].bitcast(I32),
+                x_scales[0][4 * q : 4 * q + 4, :].bitcast(I32),
+            )
+        nc.scalar.activation(warm[:, 1:2], warm[:, 0:1], ACT.Exp)
+
+        raw = {}
+        for name, w in (("w1", w1), ("w2", w2), ("w3", w3), ("w4", w4)):
+            rows = w.rearrange("(p j) c -> p j c", j=PACK)
+            for half in range(2):
+                piece = keep.tile([P, PACK, HALF], F32, name=f"raw_{name}_{half}")
+                nc.sync.dma_start(piece[:], rows[:, :, half * HALF : (half + 1) * HALF])
+                raw[(name, half)] = piece
+                if (name, half) == ("w1", 0):
+                    nc.sync.dma_start(
+                        table_words[:], x_words[0].rearrange("p c r -> p (c r)").bitcast(I32)
+                    )
+
+        picked = {}
+        for name, entries in (("src", src_list), ("dst", dst_list)):
+            words = keep.tile([P, S], U32, name=f"{name}_words", align_bytes=64)
+            scales = keep.tile([P, S], U8, name=f"{name}_scales", align_bytes=64)
+            nc.vector.tensor_copy(scales[:], table_scales[:].indirect(entries[:]))
+            picked[name] = (words, scales)
+        for name, entries in (("src", src_list), ("dst", dst_list)):
+            nc.vector.tensor_copy(picked[name][0][:], table_words[:].bitcast(U32).indirect(entries[:]))
+
+        grouped = {}
+        for name in ("w1", "w2", "w3", "w4"):
+            grouped[name] = keep.tile([P, PACK, P, PACK], BF16, name=f"grouped_{name}", align_bytes=64)
+
+        def round_half(name, half, on_vector):
+            m0 = half * (P // 2)
+            target = grouped[name][:, :, m0 : m0 + P // 2, :].rearrange("p t m j -> p m j t")
+            source = raw[(name, half)][:].rearrange("p j (m t) -> p m j t", t=PACK)
+            if on_vector:
+                nc.vector.tensor_copy(target, source)
+            else:
+                nc.scalar.copy(target, source)
+
+        weights = {}
+
+        def quantise_weight(name, pieces):
+            words = keep.tile([P, PACK * P], U32, name=f"{name}_words", align_bytes=64)
+            scales = keep.tile([P, PACK * P], U8, name=f"{name}_scales", align_bytes=64)
+            flat = grouped[name][:].rearrange("p t m j -> p (t m j)")
+            width = PACK * P // pieces
+            for n in range(pieces):
+                nc.vector.quantize_mx(
+                    out=words[:, n * width : (n + 1) * width].bitcast(FP8X4),
+                    scales=scales[:, n * width : (n + 1) * width],
+                    in_=flat[:, PACK * n * width : PACK * (n + 1) * width],
+                )
+            weights[name] = (words, scales)
+
+        def product(bank, terms, cols):
+            for t in range(PACK):
+                tile_cols = slice(t * P, (t + 1) * P)
+                for n, (name, (words, scales)) in enumerate(terms):
+                    w_words, w_scales = weights[name]
+                    nc.tensor.matmul_mx(
+                        out=bank[:, t, :],
+                        lhsT=w_words[:, tile_cols].bitcast(FP8X4),
+                        lhsT_scale=w_scales[:, tile_cols],
+                        rhs=words[:, cols].bitcast(FP8X4),
+                        rhs_scale=scales[:, cols],
+                        start=(n == 0),
+                        stop=(n == len(terms) - 1),
+                    )
+
+        round_half("w1", 0, False)
+        round_half("w1", 1, False)
+        quantise_weight("w1", 1)
+        round_half("w2", 0, False)
+        round_half("w2", 1, True)
+        quantise_weight("w2", 4)
+
+        hidden = {}
+
+        def hidden_chunk(c):
+            cols = slice(c * CHUNK, (c + 1) * CHUNK)
+            y = psum.tile([P, PACK, CHUNK], F32, name=f"y{c}")
+            product(y, (("w1", picked["src"]), ("w2", picked["dst"])), cols)
+            y_woven = y[:].rearrange("p t n -> p n t")
+            sloped = keep.tile([P, CHUNK, PACK], F32, name=f"sloped{c}")
+            nc.scalar.activation(sloped[:], y_woven, ACT.Copy, scale=SLOPE)
+            h = keep.tile([P, CHUNK, PACK], BF16, name=f"h{c}", align_bytes=64)
+            nc.vector.tensor_tensor(h[:], y_woven, sloped[:], ALU.max)
+            hidden[c] = h
+
+        h_planes = {}
+
+        def quantise_hidden(c):
+            words = keep.tile([P, CHUNK], U32, name=f"h_words{c}", align_bytes=64)
+            scales = keep.tile([P, CHUNK], U8, name=f"h_scales{c}", align_bytes=64)
+            nc.vector.quantize_mx(
+                out=words[:].bitcast(FP8X4),
+                scales=scales[:],
+                in_=hidden[c][:].rearrange("p n t -> p (n t)"),
+            )
+            h_planes[c] = (words, scales)
+
+        out_rows = out_0.rearrange("(p t) n -> p t n", t=PACK)
+        out_words = keep.tile([P, S], U32, name="out_words", align_bytes=64)
+        out_scales = keep.tile([P, S], U8, name="out_scales", align_bytes=64)
+        out_words_dram = out_1[0].rearrange("p c r -> p (c r)").bitcast(I32)
+        message = {}
+        rounded = {}
+
+        def message_chunk(c):
+            cols = slice(c * CHUNK, (c + 1) * CHUNK)
+            score = psum.tile([P, PACK, CHUNK], F32, name=f"score{c}", tag=f"score{c % 2}")
+            product(score, (("w3", h_planes[c]),), slice(0, CHUNK))
+            value = psum.tile([P, PACK, CHUNK], F32, name=f"value{c}", tag=f"value{c % 2}")
+            product(value, (("w4", picked["src"]),), cols)
+            e = keep.tile([P, PACK, CHUNK], F32, name=f"e{c}")
+            nc.scalar.activation(e[:], score[:], ACT.Exp)
+            result = keep.tile([P, PACK, CHUNK], F32, name=f"result{c}")
+            nc.vector.tensor_tensor(result[:], value[:], e[:], ALU.mult)
+            nc.sync.dma_start(out_rows[:, :, cols], result[:])
+            message[c] = result
+
+        def round_message(c, on_vector):
+            woven = keep.tile([P, CHUNK, PACK], BF16, name=f"woven{c}", align_bytes=64)
+            target = woven[:].rearrange("p (g i) t -> p g t i", i=4)
+            source = message[c][:].rearrange("p t (g i) -> p g t i", i=4)
+            if on_vector:
+                nc.vector.tensor_copy(target, source)
+            else:
+                nc.scalar.copy(target, source)
+            rounded[c] = woven
+
+        def quantise_message(c):
+            cols = slice(c * CHUNK, (c + 1) * CHUNK)
+            nc.vector.quantize_mx(
+                out=out_words[:, cols].bitcast(FP8X4),
+                scales=out_scales[:, cols],
+                in_=rounded[c][:].rearrange("p n t -> p (n t)"),
+            )
+            nc.sync.dma_start(out_words_dram[:, cols], out_words[:, cols].bitcast(I32))
+
+        round_half("w3", 0, False)
+        round_half("w3", 1, True)
+        hidden_chunk(0)
+        quantise_weight("w3", 1)
+        hidden_chunk(1)
+        quantise_hidden(0)
+        hidden_chunk(2)
+        quantise_hidden(1)
+        hidden_chunk(3)
+        quantise_hidden(2)
+        round_half("w4", 0, False)
+        round_half("w4", 1, True)
+        quantise_hidden(3)
+        quantise_weight("w4", 2)
+        for c in range(CHUNKS):
+            message_chunk(c)
+            if c > 0:
+                quantise_message(c - 1)
+            round_message(c, c == CHUNKS - 1)
+        quantise_message(CHUNKS - 1)
+        for q in range(4):
+            queue = nc.scalar if q % 2 else nc.sync
+            queue.dma_start(
+                out_2[0][4 * q : 4 * q + 4, :].bitcast(I32),
+                out_scales[32 * q : 32 * q + 4, :].bitcast(I32),
+            )

@@ -21,6 +21,7 @@ CHUNK = 128
 CHUNKS = S // CHUNK
 HALF = 256
 SLOPE = 0.2
+WARM_PASSES = 4
 
 
 def tile_picked_zgatt_exp_po_kernel(
@@ -40,6 +41,7 @@ def tile_picked_zgatt_exp_po_kernel(
         warm = keep.tile([P, 2], F32, name="warm")
         nc.vector.memset(warm[:, 0:1], 0.0)
 
+        nc.sync.dma_start(table_words[:], x_words[0].rearrange("p c r -> p (c r)").bitcast(I32))
         nc.sync.dma_start(src_list[:], offs)
         nc.sync.dma_start(dst_list[:], dst)
         for q in range(4):
@@ -56,19 +58,28 @@ def tile_picked_zgatt_exp_po_kernel(
                 piece = keep.tile([P, PACK, HALF], F32, name=f"raw_{name}_{half}")
                 nc.sync.dma_start(piece[:], rows[:, :, half * HALF : (half + 1) * HALF])
                 raw[(name, half)] = piece
-                if (name, half) == ("w1", 0):
-                    nc.sync.dma_start(
-                        table_words[:], x_words[0].rearrange("p c r -> p (c r)").bitcast(I32)
-                    )
 
         picked = {}
         for name, entries in (("src", src_list), ("dst", dst_list)):
             words = keep.tile([P, S], U32, name=f"{name}_words", align_bytes=64)
             scales = keep.tile([P, S], U8, name=f"{name}_scales", align_bytes=64)
-            nc.vector.tensor_copy(scales[:], table_scales[:].indirect(entries[:]))
+            nc.vector.tensor_copy(words[:], table_words[:].bitcast(U32).indirect(entries[:]))
             picked[name] = (words, scales)
         for name, entries in (("src", src_list), ("dst", dst_list)):
-            nc.vector.tensor_copy(picked[name][0][:], table_words[:].bitcast(U32).indirect(entries[:]))
+            nc.vector.tensor_copy(picked[name][1][:], table_scales[:].indirect(entries[:]))
+
+        src_words, src_scales = picked["src"]
+        idle_bank = psum.tile([P, S], F32, name="idle_bank", tag="value1")
+        for n in range(WARM_PASSES):
+            nc.tensor.matmul_mx(
+                out=idle_bank[:],
+                lhsT=src_words[:, 0:P].bitcast(FP8X4),
+                lhsT_scale=src_scales[:, 0:P],
+                rhs=src_words[:].bitcast(FP8X4),
+                rhs_scale=src_scales[:],
+                start=True,
+                stop=True,
+            )
 
         grouped = {}
         for name in ("w1", "w2", "w3", "w4"):
@@ -117,46 +128,42 @@ def tile_picked_zgatt_exp_po_kernel(
         round_half("w1", 1, False)
         quantise_weight("w1", 1)
         round_half("w2", 0, False)
-        round_half("w2", 1, True)
-        quantise_weight("w2", 4)
+        round_half("w2", 1, False)
+        quantise_weight("w2", 2)
 
-        hidden = {}
+        hidden = keep.tile([P, S, PACK], BF16, name="hidden", align_bytes=64)
+        h_words = keep.tile([P, S], U32, name="h_words", align_bytes=64)
+        h_scales = keep.tile([P, S], U8, name="h_scales", align_bytes=64)
 
         def hidden_chunk(c):
             cols = slice(c * CHUNK, (c + 1) * CHUNK)
-            y = psum.tile([P, PACK, CHUNK], F32, name=f"y{c}")
+            y = psum.tile([P, PACK, CHUNK], F32, name=f"y{c}", tag=f"y{c}")
             product(y, (("w1", picked["src"]), ("w2", picked["dst"])), cols)
             y_woven = y[:].rearrange("p t n -> p n t")
             sloped = keep.tile([P, CHUNK, PACK], F32, name=f"sloped{c}")
             nc.scalar.activation(sloped[:], y_woven, ACT.Copy, scale=SLOPE)
-            h = keep.tile([P, CHUNK, PACK], BF16, name=f"h{c}", align_bytes=64)
-            nc.vector.tensor_tensor(h[:], y_woven, sloped[:], ALU.max)
-            hidden[c] = h
+            nc.vector.tensor_tensor(hidden[:, cols, :], y_woven, sloped[:], ALU.max)
 
-        h_planes = {}
-
-        def quantise_hidden(c):
-            words = keep.tile([P, CHUNK], U32, name=f"h_words{c}", align_bytes=64)
-            scales = keep.tile([P, CHUNK], U8, name=f"h_scales{c}", align_bytes=64)
+        def quantise_hidden(first, count):
+            cols = slice(first * CHUNK, (first + count) * CHUNK)
             nc.vector.quantize_mx(
-                out=words[:].bitcast(FP8X4),
-                scales=scales[:],
-                in_=hidden[c][:].rearrange("p n t -> p (n t)"),
+                out=h_words[:, cols].bitcast(FP8X4),
+                scales=h_scales[:, cols],
+                in_=hidden[:, cols, :].rearrange("p n t -> p (n t)"),
             )
-            h_planes[c] = (words, scales)
 
         out_rows = out_0.rearrange("(p t) n -> p t n", t=PACK)
         out_words = keep.tile([P, S], U32, name="out_words", align_bytes=64)
         out_scales = keep.tile([P, S], U8, name="out_scales", align_bytes=64)
         out_words_dram = out_1[0].rearrange("p c r -> p (c r)").bitcast(I32)
         message = {}
-        rounded = {}
+        rounded = keep.tile([P, S, PACK], BF16, name="rounded", align_bytes=64)
 
         def message_chunk(c):
             cols = slice(c * CHUNK, (c + 1) * CHUNK)
-            score = psum.tile([P, PACK, CHUNK], F32, name=f"score{c}", tag=f"score{c % 2}")
-            product(score, (("w3", h_planes[c]),), slice(0, CHUNK))
-            value = psum.tile([P, PACK, CHUNK], F32, name=f"value{c}", tag=f"value{c % 2}")
+            score = psum.tile([P, PACK, CHUNK], F32, name=f"score{c}", tag=f"score{c}" if c < 2 else f"y{c - 2}")
+            product(score, (("w3", (h_words, h_scales)),), cols)
+            value = psum.tile([P, PACK, CHUNK], F32, name=f"value{c}", tag=f"value{c}" if c < 2 else f"y{c}")
             product(value, (("w4", picked["src"]),), cols)
             e = keep.tile([P, PACK, CHUNK], F32, name=f"e{c}")
             nc.scalar.activation(e[:], score[:], ACT.Exp)
@@ -166,21 +173,19 @@ def tile_picked_zgatt_exp_po_kernel(
             message[c] = result
 
         def round_message(c, on_vector):
-            woven = keep.tile([P, CHUNK, PACK], BF16, name=f"woven{c}", align_bytes=64)
-            target = woven[:].rearrange("p (g i) t -> p g t i", i=4)
+            target = rounded[:, c * CHUNK : (c + 1) * CHUNK, :].rearrange("p (g i) t -> p g t i", i=4)
             source = message[c][:].rearrange("p t (g i) -> p g t i", i=4)
             if on_vector:
                 nc.vector.tensor_copy(target, source)
             else:
                 nc.scalar.copy(target, source)
-            rounded[c] = woven
 
-        def quantise_message(c):
-            cols = slice(c * CHUNK, (c + 1) * CHUNK)
+        def quantise_message(first, count):
+            cols = slice(first * CHUNK, (first + count) * CHUNK)
             nc.vector.quantize_mx(
                 out=out_words[:, cols].bitcast(FP8X4),
                 scales=out_scales[:, cols],
-                in_=rounded[c][:].rearrange("p n t -> p (n t)"),
+                in_=rounded[:, cols, :].rearrange("p n t -> p (n t)"),
             )
             nc.sync.dma_start(out_words_dram[:, cols], out_words[:, cols].bitcast(I32))
 
@@ -189,21 +194,23 @@ def tile_picked_zgatt_exp_po_kernel(
         hidden_chunk(0)
         quantise_weight("w3", 1)
         hidden_chunk(1)
-        quantise_hidden(0)
+        quantise_hidden(0, 1)
         hidden_chunk(2)
-        quantise_hidden(1)
+        quantise_hidden(1, 1)
         hidden_chunk(3)
-        quantise_hidden(2)
         round_half("w4", 0, False)
         round_half("w4", 1, True)
-        quantise_hidden(3)
         quantise_weight("w4", 2)
+        quantise_hidden(2, 1)
+        quantise_hidden(3, 1)
         for c in range(CHUNKS):
             message_chunk(c)
-            if c > 0:
-                quantise_message(c - 1)
-            round_message(c, c == CHUNKS - 1)
-        quantise_message(CHUNKS - 1)
+        round_message(0, False)
+        round_message(1, False)
+        quantise_message(0, 2)
+        round_message(2, False)
+        round_message(3, True)
+        quantise_message(2, 2)
         for q in range(4):
             queue = nc.scalar if q % 2 else nc.sync
             queue.dma_start(

@@ -53,11 +53,8 @@ def tile_picked_zgatt_exp_po_kernel(
 
         raw = {}
         for name, w in (("w1", w1), ("w2", w2), ("w3", w3), ("w4", w4)):
-            rows = w.rearrange("(p j) c -> p j c", j=PACK)
-            for half in range(2):
-                piece = keep.tile([P, PACK, HALF], F32, name=f"raw_{name}_{half}")
-                nc.sync.dma_start(piece[:], rows[:, :, half * HALF : (half + 1) * HALF])
-                raw[(name, half)] = piece
+            raw[name] = keep.tile([P, PACK, H], F32, name=f"raw_{name}")
+            nc.sync.dma_start(raw[name][:], w.rearrange("(p j) c -> p j c", j=PACK))
 
         picked = {}
         for name, entries in (("src", src_list), ("dst", dst_list)):
@@ -85,11 +82,12 @@ def tile_picked_zgatt_exp_po_kernel(
         for name in ("w1", "w2", "w3", "w4"):
             grouped[name] = keep.tile([P, PACK, P, PACK], BF16, name=f"grouped_{name}", align_bytes=64)
 
-        def round_half(name, half, on_vector):
-            m0 = half * (P // 2)
-            target = grouped[name][:, :, m0 : m0 + P // 2, :].rearrange("p t m j -> p m j t")
-            source = raw[(name, half)][:].rearrange("p j (m t) -> p m j t", t=PACK)
-            if on_vector:
+        def round_columns(name, first, count, engine):
+            target = grouped[name][:, :, first : first + count, :].rearrange("p t m j -> p m j t")
+            source = raw[name][:, :, PACK * first : PACK * (first + count)].rearrange(
+                "p j (m t) -> p m j t", t=PACK
+            )
+            if engine == "vector":
                 nc.vector.tensor_copy(target, source)
             else:
                 nc.scalar.copy(target, source)
@@ -124,11 +122,10 @@ def tile_picked_zgatt_exp_po_kernel(
                         stop=(n == len(terms) - 1),
                     )
 
-        round_half("w1", 0, False)
-        round_half("w1", 1, False)
+        round_columns("w1", 0, 128, "scalar")
+        round_columns("w2", 64, 64, "vector")
         quantise_weight("w1", 1)
-        round_half("w2", 0, False)
-        round_half("w2", 1, False)
+        round_columns("w2", 0, 64, "scalar")
         quantise_weight("w2", 2)
 
         hidden = keep.tile([P, S, PACK], BF16, name="hidden", align_bytes=64)
@@ -189,19 +186,19 @@ def tile_picked_zgatt_exp_po_kernel(
             )
             nc.sync.dma_start(out_words_dram[:, cols], out_words[:, cols].bitcast(I32))
 
-        round_half("w3", 0, False)
-        round_half("w3", 1, True)
+        round_columns("w3", 0, 48, "scalar")
+        round_columns("w3", 48, 80, "vector")
         hidden_chunk(0)
         quantise_weight("w3", 1)
         hidden_chunk(1)
         quantise_hidden(0, 1)
         hidden_chunk(2)
         quantise_hidden(1, 1)
+        round_columns("w4", 80, 48, "vector")
         hidden_chunk(3)
-        round_half("w4", 0, False)
-        round_half("w4", 1, True)
-        quantise_weight("w4", 2)
         quantise_hidden(2, 1)
+        round_columns("w4", 0, 80, "scalar")
+        quantise_weight("w4", 2)
         quantise_hidden(3, 1)
         for c in range(CHUNKS):
             message_chunk(c)

@@ -18,10 +18,10 @@ ACT = mybir.ActivationFunctionType
 P = 128
 PACK = 4
 CHUNK = 128
-CHUNKS = S // CHUNK
-HALF = 256
 SLOPE = 0.2
 WARM_PASSES = 4
+SCORE_BANK = ("a", "b", "y0", "y1")
+VALUE_BANK = ("c", "value1", "y2", "a")
 
 
 def tile_picked_zgatt_exp_po_kernel(
@@ -52,60 +52,69 @@ def tile_picked_zgatt_exp_po_kernel(
         nc.scalar.activation(warm[:, 1:2], warm[:, 0:1], ACT.Exp)
 
         raw = {}
-        for name, w in (("w1", w1), ("w2", w2), ("w3", w3), ("w4", w4)):
-            raw[name] = keep.tile([P, PACK, H], F32, name=f"raw_{name}")
-            nc.sync.dma_start(raw[name][:], w.rearrange("(p j) c -> p j c", j=PACK))
+        for name, w, cuts in (("w1", w1, (0, 128)), ("w2", w2, (0, 128)), ("w3", w3, (0, 128)), ("w4", w4, (0, 128))):
+            raw[name] = []
+            rows = w.rearrange("(p j) c -> p j c", j=PACK)
+            for first, last in zip(cuts, cuts[1:]):
+                tile = keep.tile([P, PACK, PACK * (last - first)], F32, name=f"raw_{name}_{first}")
+                nc.sync.dma_start(tile[:], rows[:, :, PACK * first : PACK * last])
+                raw[name].append((first, tile))
 
         picked = {}
-        for name, entries in (("src", src_list), ("dst", dst_list)):
+        for name in ("src", "dst"):
             words = keep.tile([P, S], U32, name=f"{name}_words", align_bytes=64)
             scales = keep.tile([P, S], U8, name=f"{name}_scales", align_bytes=64)
-            nc.vector.tensor_copy(words[:], table_words[:].bitcast(U32).indirect(entries[:]))
             picked[name] = (words, scales)
+        for name, entries in (("src", src_list), ("dst", dst_list)):
+            nc.vector.tensor_copy(picked[name][0][:], table_words[:].bitcast(U32).indirect(entries[:]))
         for name, entries in (("src", src_list), ("dst", dst_list)):
             nc.vector.tensor_copy(picked[name][1][:], table_scales[:].indirect(entries[:]))
 
-        src_words, src_scales = picked["src"]
-        idle_bank = psum.tile([P, S], F32, name="idle_bank", tag="value1")
-        for n in range(WARM_PASSES):
-            nc.tensor.matmul_mx(
-                out=idle_bank[:],
-                lhsT=src_words[:, 0:P].bitcast(FP8X4),
-                lhsT_scale=src_scales[:, 0:P],
-                rhs=src_words[:].bitcast(FP8X4),
-                rhs_scale=src_scales[:],
-                start=True,
-                stop=True,
-            )
+
+        def warm_up(name, passes, bank):
+            words, scales = picked[name]
+            idle_bank = psum.tile([P, S], F32, name=f"idle_{bank}", tag=bank)
+            for n in range(passes):
+                nc.tensor.matmul_mx(
+                    out=idle_bank[:],
+                    lhsT=words[:, 0:P].bitcast(FP8X4),
+                    lhsT_scale=scales[:, 0:P],
+                    rhs=words[:].bitcast(FP8X4),
+                    rhs_scale=scales[:],
+                    start=True,
+                    stop=True,
+                )
 
         grouped = {}
+        weights = {}
         for name in ("w1", "w2", "w3", "w4"):
             grouped[name] = keep.tile([P, PACK, P, PACK], BF16, name=f"grouped_{name}", align_bytes=64)
+            words = keep.tile([P, PACK * P], U32, name=f"{name}_words", align_bytes=64)
+            scales = keep.tile([P, PACK * P], U8, name=f"{name}_scales", align_bytes=64)
+            weights[name] = (words, scales)
 
-        def round_columns(name, first, count, engine):
-            target = grouped[name][:, :, first : first + count, :].rearrange("p t m j -> p m j t")
-            source = raw[name][:, :, PACK * first : PACK * (first + count)].rearrange(
-                "p j (m t) -> p m j t", t=PACK
-            )
+        def convert(target, source, engine):
             if engine == "vector":
                 nc.vector.tensor_copy(target, source)
+            elif engine == "gpsimd":
+                nc.gpsimd.tensor_scalar(target, source, 1.0, 0.0, ALU.mult, ALU.add)
             else:
                 nc.scalar.copy(target, source)
 
-        weights = {}
+        def round_weight(name, tiles, first, last, engine):
+            start, tile = [piece for piece in raw[name] if piece[0] <= first][-1]
+            target = grouped[name][:, tiles, first:last, :].rearrange("p t m j -> p m j t")
+            source = tile[:].rearrange("p j (m t) -> p t m j", t=PACK)[:, tiles, first - start : last - start, :]
+            convert(target, source.rearrange("p t m j -> p m j t"), engine)
 
-        def quantise_weight(name, pieces):
-            words = keep.tile([P, PACK * P], U32, name=f"{name}_words", align_bytes=64)
-            scales = keep.tile([P, PACK * P], U8, name=f"{name}_scales", align_bytes=64)
+        def quantise_tiles(name, first, last):
+            words, scales = weights[name]
             flat = grouped[name][:].rearrange("p t m j -> p (t m j)")
-            width = PACK * P // pieces
-            for n in range(pieces):
-                nc.vector.quantize_mx(
-                    out=words[:, n * width : (n + 1) * width].bitcast(FP8X4),
-                    scales=scales[:, n * width : (n + 1) * width],
-                    in_=flat[:, PACK * n * width : PACK * (n + 1) * width],
-                )
-            weights[name] = (words, scales)
+            nc.vector.quantize_mx(
+                out=words[:, first * P : last * P].bitcast(FP8X4),
+                scales=scales[:, first * P : last * P],
+                in_=flat[:, PACK * first * P : PACK * last * P],
+            )
 
         def product(bank, terms, cols):
             for t in range(PACK):
@@ -122,24 +131,23 @@ def tile_picked_zgatt_exp_po_kernel(
                         stop=(n == len(terms) - 1),
                     )
 
-        round_columns("w1", 0, 128, "scalar")
-        round_columns("w2", 64, 64, "vector")
-        quantise_weight("w1", 1)
-        round_columns("w2", 0, 64, "scalar")
-        quantise_weight("w2", 2)
-
         hidden = keep.tile([P, S, PACK], BF16, name="hidden", align_bytes=64)
         h_words = keep.tile([P, S], U32, name="h_words", align_bytes=64)
         h_scales = keep.tile([P, S], U8, name="h_scales", align_bytes=64)
+        sums, sloped, scores, values, exps, message = {}, {}, {}, {}, {}, {}
 
-        def hidden_chunk(c):
+        def sum_chunk(c):
             cols = slice(c * CHUNK, (c + 1) * CHUNK)
-            y = psum.tile([P, PACK, CHUNK], F32, name=f"y{c}", tag=f"y{c}")
-            product(y, (("w1", picked["src"]), ("w2", picked["dst"])), cols)
-            y_woven = y[:].rearrange("p t n -> p n t")
-            sloped = keep.tile([P, CHUNK, PACK], F32, name=f"sloped{c}")
-            nc.scalar.activation(sloped[:], y_woven, ACT.Copy, scale=SLOPE)
-            nc.vector.tensor_tensor(hidden[:, cols, :], y_woven, sloped[:], ALU.max)
+            sums[c] = psum.tile([P, PACK, CHUNK], F32, name=f"y{c}", tag=f"y{c}")
+            product(sums[c], (("w1", picked["src"]), ("w2", picked["dst"])), cols)
+
+        def slope_chunk(c):
+            sloped[c] = keep.tile([P, CHUNK, PACK], F32, name=f"sloped{c}")
+            nc.scalar.activation(sloped[c][:], sums[c][:].rearrange("p t n -> p n t"), ACT.Copy, scale=SLOPE)
+
+        def leaky_chunk(c):
+            cols = slice(c * CHUNK, (c + 1) * CHUNK)
+            nc.vector.tensor_tensor(hidden[:, cols, :], sums[c][:].rearrange("p t n -> p n t"), sloped[c][:], ALU.max)
 
         def quantise_hidden(first, count):
             cols = slice(first * CHUNK, (first + count) * CHUNK)
@@ -153,29 +161,32 @@ def tile_picked_zgatt_exp_po_kernel(
         out_words = keep.tile([P, S], U32, name="out_words", align_bytes=64)
         out_scales = keep.tile([P, S], U8, name="out_scales", align_bytes=64)
         out_words_dram = out_1[0].rearrange("p c r -> p (c r)").bitcast(I32)
-        message = {}
         rounded = keep.tile([P, S, PACK], BF16, name="rounded", align_bytes=64)
+
+        def score_chunk(c):
+            cols = slice(c * CHUNK, (c + 1) * CHUNK)
+            scores[c] = psum.tile([P, PACK, CHUNK], F32, name=f"score{c}", tag=SCORE_BANK[c])
+            product(scores[c], (("w3", (h_words, h_scales)),), cols)
+
+        def exp_chunk(c):
+            exps[c] = keep.tile([P, PACK, CHUNK], F32, name=f"e{c}")
+            nc.scalar.activation(exps[c][:], scores[c][:], ACT.Exp)
+
+        def value_chunk(c):
+            cols = slice(c * CHUNK, (c + 1) * CHUNK)
+            values[c] = psum.tile([P, PACK, CHUNK], F32, name=f"value{c}", tag=VALUE_BANK[c])
+            product(values[c], (("w4", picked["src"]),), cols)
 
         def message_chunk(c):
             cols = slice(c * CHUNK, (c + 1) * CHUNK)
-            score = psum.tile([P, PACK, CHUNK], F32, name=f"score{c}", tag=f"score{c}" if c < 2 else f"y{c - 2}")
-            product(score, (("w3", (h_words, h_scales)),), cols)
-            value = psum.tile([P, PACK, CHUNK], F32, name=f"value{c}", tag=f"value{c}" if c < 2 else f"y{c}")
-            product(value, (("w4", picked["src"]),), cols)
-            e = keep.tile([P, PACK, CHUNK], F32, name=f"e{c}")
-            nc.scalar.activation(e[:], score[:], ACT.Exp)
-            result = keep.tile([P, PACK, CHUNK], F32, name=f"result{c}")
-            nc.vector.tensor_tensor(result[:], value[:], e[:], ALU.mult)
-            nc.sync.dma_start(out_rows[:, :, cols], result[:])
-            message[c] = result
+            message[c] = keep.tile([P, PACK, CHUNK], F32, name=f"result{c}")
+            nc.vector.tensor_tensor(message[c][:], values[c][:], exps[c][:], ALU.mult)
+            nc.sync.dma_start(out_rows[:, :, cols], message[c][:])
 
-        def round_message(c, on_vector):
-            target = rounded[:, c * CHUNK : (c + 1) * CHUNK, :].rearrange("p (g i) t -> p g t i", i=4)
-            source = message[c][:].rearrange("p t (g i) -> p g t i", i=4)
-            if on_vector:
-                nc.vector.tensor_copy(target, source)
-            else:
-                nc.scalar.copy(target, source)
+        def round_message(c, engine, first, last):
+            target = rounded[:, c * CHUNK + first : c * CHUNK + last, :].rearrange("p (g i) t -> p g t i", i=4)
+            source = message[c][:, :, first:last].rearrange("p t (g i) -> p g t i", i=4)
+            convert(target, source, engine)
 
         def quantise_message(first, count):
             cols = slice(first * CHUNK, (first + count) * CHUNK)
@@ -184,30 +195,66 @@ def tile_picked_zgatt_exp_po_kernel(
                 scales=out_scales[:, cols],
                 in_=rounded[:, cols, :].rearrange("p n t -> p (n t)"),
             )
+
+        def store_words(first, count):
+            cols = slice(first * CHUNK, (first + count) * CHUNK)
             nc.sync.dma_start(out_words_dram[:, cols], out_words[:, cols].bitcast(I32))
 
-        round_columns("w3", 0, 48, "scalar")
-        round_columns("w3", 48, 80, "vector")
-        hidden_chunk(0)
-        quantise_weight("w3", 1)
-        hidden_chunk(1)
+        warm_up("dst", 3, "value1")
+        round_weight("w1", slice(0, 4), 0, 128, "scalar")
+        round_weight("w2", slice(0, 2), 0, 128, "vector")
+        quantise_tiles("w1", 0, 4)
+        round_weight("w2", slice(2, 4), 0, 128, "scalar")
+        quantise_tiles("w2", 0, 2)
+        quantise_tiles("w2", 2, 4)
+        round_weight("w3", slice(0, 4), 0, 40, "scalar")
+        round_weight("w3", slice(0, 4), 40, 128, "vector")
+        quantise_tiles("w3", 0, 4)
+        sum_chunk(0)
+        slope_chunk(0)
+        leaky_chunk(0)
+        sum_chunk(1)
+        slope_chunk(1)
+        leaky_chunk(1)
         quantise_hidden(0, 1)
-        hidden_chunk(2)
+        score_chunk(0)
+        sum_chunk(2)
+        slope_chunk(2)
+        leaky_chunk(2)
         quantise_hidden(1, 1)
-        round_columns("w4", 80, 48, "vector")
-        hidden_chunk(3)
+        score_chunk(1)
+        sum_chunk(3)
+        slope_chunk(3)
+        round_weight("w4", slice(0, 4), 0, 64, "scalar")
+        round_weight("w4", slice(0, 4), 64, 128, "vector")
         quantise_hidden(2, 1)
-        round_columns("w4", 0, 80, "scalar")
-        quantise_weight("w4", 2)
+        score_chunk(2)
+        quantise_tiles("w4", 0, 4)
+        value_chunk(0)
+        value_chunk(1)
+        leaky_chunk(3)
         quantise_hidden(3, 1)
-        for c in range(CHUNKS):
-            message_chunk(c)
-        round_message(0, False)
-        round_message(1, False)
+        exp_chunk(0)
+        exp_chunk(1)
+        exp_chunk(2)
+        score_chunk(3)
+        exp_chunk(3)
+        value_chunk(2)
+        value_chunk(3)
+        message_chunk(0)
+        message_chunk(1)
+        message_chunk(2)
+        message_chunk(3)
+        round_message(1, "scalar", 0, 128)
+        round_message(2, "scalar", 0, 128)
+        round_message(0, "vector", 0, 128)
+        round_message(3, "vector", 64, 128)
+        round_message(3, "scalar", 0, 64)
         quantise_message(0, 2)
-        round_message(2, False)
-        round_message(3, True)
+        store_words(0, 2)
         quantise_message(2, 2)
+        store_words(2, 2)
+
         for q in range(4):
             queue = nc.scalar if q % 2 else nc.sync
             queue.dma_start(

@@ -20,7 +20,8 @@ PACK = 4
 CHUNK = 128
 SLOPE = 0.2
 WARM_PASSES = 4
-SCORE_BANK = ("a", "b", "y0", "y1")
+SUM_BANK = ("y0", "y1", "y2", "y0")
+SCORE_BANK = ("a", "b", "y1", "d")
 VALUE_BANK = ("c", "value1", "y2", "a")
 
 
@@ -56,7 +57,7 @@ def tile_picked_zgatt_exp_po_kernel(
             raw[name] = []
             rows = w.rearrange("(p j) c -> p j c", j=PACK)
             for first, last in zip(cuts, cuts[1:]):
-                tile = keep.tile([P, PACK, PACK * (last - first)], F32, name=f"raw_{name}_{first}")
+                tile = keep.tile([P, PACK, PACK * (last - first)], F32, name=f"raw_{name}_{first}", tag=f"raw_{name}_{first}")
                 nc.sync.dma_start(tile[:], rows[:, :, PACK * first : PACK * last])
                 raw[name].append((first, tile))
 
@@ -138,11 +139,11 @@ def tile_picked_zgatt_exp_po_kernel(
 
         def sum_chunk(c):
             cols = slice(c * CHUNK, (c + 1) * CHUNK)
-            sums[c] = psum.tile([P, PACK, CHUNK], F32, name=f"y{c}", tag=f"y{c}")
+            sums[c] = psum.tile([P, PACK, CHUNK], F32, name=f"y{c}", tag=SUM_BANK[c])
             product(sums[c], (("w1", picked["src"]), ("w2", picked["dst"])), cols)
 
         def slope_chunk(c):
-            sloped[c] = keep.tile([P, CHUNK, PACK], F32, name=f"sloped{c}")
+            sloped[c] = keep.tile([P, CHUNK, PACK], F32, name=f"sloped{c}", tag="raw_w4_0" if c == 3 else f"sloped{c}")
             nc.scalar.activation(sloped[c][:], sums[c][:].rearrange("p t n -> p n t"), ACT.Copy, scale=SLOPE)
 
         def leaky_chunk(c):
@@ -221,38 +222,39 @@ def tile_picked_zgatt_exp_po_kernel(
         sum_chunk(2)
         slope_chunk(2)
         leaky_chunk(2)
+        sum_chunk(3)
+        round_weight("w4", slice(0, 4), 0, 88, "scalar")
+        round_weight("w4", slice(0, 4), 88, 128, "vector")
         quantise_hidden(1, 1)
         score_chunk(1)
-        sum_chunk(3)
-        slope_chunk(3)
-        round_weight("w4", slice(0, 4), 0, 64, "scalar")
-        round_weight("w4", slice(0, 4), 64, 128, "vector")
-        quantise_hidden(2, 1)
-        score_chunk(2)
         quantise_tiles("w4", 0, 4)
         value_chunk(0)
+        quantise_hidden(2, 1)
+        score_chunk(2)
         value_chunk(1)
+        slope_chunk(3)
         leaky_chunk(3)
-        quantise_hidden(3, 1)
         exp_chunk(0)
         exp_chunk(1)
         exp_chunk(2)
+        message_chunk(0)
+        quantise_hidden(3, 1)
         score_chunk(3)
         exp_chunk(3)
         value_chunk(2)
         value_chunk(3)
-        message_chunk(0)
         message_chunk(1)
         message_chunk(2)
         message_chunk(3)
-        round_message(1, "scalar", 0, 128)
+        round_message(0, "scalar", 0, 128)
+        round_message(1, "vector", 0, 128)
         round_message(2, "scalar", 0, 128)
-        round_message(0, "vector", 0, 128)
-        round_message(3, "vector", 64, 128)
-        round_message(3, "scalar", 0, 64)
         quantise_message(0, 2)
         store_words(0, 2)
-        quantise_message(2, 2)
+        round_message(3, "vector", 48, 128)
+        round_message(3, "scalar", 0, 48)
+        quantise_message(2, 1)
+        quantise_message(3, 1)
         store_words(2, 2)
 
         for q in range(4):

@@ -20,9 +20,9 @@ PACK = 4
 CHUNK = 128
 SLOPE = 0.2
 WARM_PASSES = 4
-SUM_BANK = ("y0", "y1", "y2", "y0")
-SCORE_BANK = ("a", "b", "y1", "d")
-VALUE_BANK = ("c", "value1", "y2", "a")
+SUM_BANK = ("y0", "y1", "y2", "y3")
+SCORE_BANK = ("y0", "y1", "y2", "y3")
+VALUE_BANK = ("v0", "v1", "v2", "v3")
 
 
 def tile_picked_zgatt_exp_po_kernel(
@@ -31,6 +31,7 @@ def tile_picked_zgatt_exp_po_kernel(
     nc = tc.nc
     with ExitStack() as ctx:
         keep = ctx.enter_context(tc.tile_pool(name="keep", bufs=1))
+        reuse = ctx.enter_context(tc.tile_pool(name="reuse", bufs=1))
         psum = ctx.enter_context(tc.psum_pool(name="psum", bufs=1))
 
         table_words = keep.tile([P, T], I32, name="table_words")
@@ -53,7 +54,7 @@ def tile_picked_zgatt_exp_po_kernel(
         nc.scalar.activation(warm[:, 1:2], warm[:, 0:1], ACT.Exp)
 
         raw = {}
-        for name, w, cuts in (("w1", w1, (0, 128)), ("w2", w2, (0, 128)), ("w3", w3, (0, 128)), ("w4", w4, (0, 128))):
+        for name, w, cuts in (("w1", w1, (0, 128)), ("w4", w4, (0, 128)), ("w2", w2, (0, 128)), ("w3", w3, (0, 128))):
             raw[name] = []
             rows = w.rearrange("(p j) c -> p j c", j=PACK)
             for first, last in zip(cuts, cuts[1:]):
@@ -89,7 +90,10 @@ def tile_picked_zgatt_exp_po_kernel(
         grouped = {}
         weights = {}
         for name in ("w1", "w2", "w3", "w4"):
-            grouped[name] = keep.tile([P, PACK, P, PACK], BF16, name=f"grouped_{name}", align_bytes=64)
+            if name == "w3":
+                grouped[name] = reuse.tile([P, PACK, P, PACK], BF16, name="grouped_w3", offset=0, align_bytes=64)
+            else:
+                grouped[name] = keep.tile([P, PACK, P, PACK], BF16, name=f"grouped_{name}", align_bytes=64)
             words = keep.tile([P, PACK * P], U32, name=f"{name}_words", align_bytes=64)
             scales = keep.tile([P, PACK * P], U8, name=f"{name}_scales", align_bytes=64)
             weights[name] = (words, scales)
@@ -135,7 +139,7 @@ def tile_picked_zgatt_exp_po_kernel(
         hidden = keep.tile([P, S, PACK], BF16, name="hidden", align_bytes=64)
         h_words = keep.tile([P, S], U32, name="h_words", align_bytes=64)
         h_scales = keep.tile([P, S], U8, name="h_scales", align_bytes=64)
-        sums, sloped, scores, values, exps, message = {}, {}, {}, {}, {}, {}
+        sums, plain, sloped, scores, values, exps, message = {}, {}, {}, {}, {}, {}, {}
 
         def sum_chunk(c):
             cols = slice(c * CHUNK, (c + 1) * CHUNK)
@@ -143,12 +147,20 @@ def tile_picked_zgatt_exp_po_kernel(
             product(sums[c], (("w1", picked["src"]), ("w2", picked["dst"])), cols)
 
         def slope_chunk(c):
-            sloped[c] = keep.tile([P, CHUNK, PACK], F32, name=f"sloped{c}", tag="raw_w4_0" if c == 3 else f"sloped{c}")
-            nc.scalar.activation(sloped[c][:], sums[c][:].rearrange("p t n -> p n t"), ACT.Copy, scale=SLOPE)
+            rows = raw["w3"][0][1][:, :, c * CHUNK : (c + 1) * CHUNK]
+            if c == 3:
+                both = reuse.tile([P, 2, PACK, CHUNK // PACK, PACK], BF16, name="both", offset=0, align_bytes=64)
+                plain[c], sloped[c] = both[:, 0], both[:, 1]
+                nc.scalar.copy(plain[c], sums[c][:].rearrange("p t (r n) -> p r n t", r=PACK))
+            else:
+                plain[c] = sums[c][:].rearrange("p t (r n) -> p r n t", r=PACK)
+                sloped[c] = rows.rearrange("p r (n t) -> p r n t", t=PACK)
+            nc.scalar.activation(sloped[c], sums[c][:].rearrange("p t (r n) -> p r n t", r=PACK), ACT.Copy, scale=SLOPE)
 
         def leaky_chunk(c):
             cols = slice(c * CHUNK, (c + 1) * CHUNK)
-            nc.vector.tensor_tensor(hidden[:, cols, :], sums[c][:].rearrange("p t n -> p n t"), sloped[c][:], ALU.max)
+            target = hidden[:, cols, :].rearrange("p (r n) t -> p r n t", r=PACK)
+            nc.vector.tensor_tensor(target, plain[c], sloped[c], ALU.max)
 
         def quantise_hidden(first, count):
             cols = slice(first * CHUNK, (first + count) * CHUNK)
@@ -201,54 +213,45 @@ def tile_picked_zgatt_exp_po_kernel(
             cols = slice(first * CHUNK, (first + count) * CHUNK)
             nc.sync.dma_start(out_words_dram[:, cols], out_words[:, cols].bitcast(I32))
 
-        warm_up("dst", 3, "value1")
+        warm_up("dst", 2, "y3")
         round_weight("w1", slice(0, 4), 0, 128, "scalar")
-        round_weight("w2", slice(0, 2), 0, 128, "vector")
         quantise_tiles("w1", 0, 4)
-        round_weight("w2", slice(2, 4), 0, 128, "scalar")
+        round_weight("w4", slice(0, 4), 0, 76, "scalar")
+        round_weight("w4", slice(0, 4), 76, 128, "vector")
+        quantise_tiles("w4", 0, 4)
+        round_weight("w2", slice(0, 2), 0, 128, "scalar")
+        round_weight("w2", slice(2, 4), 0, 128, "vector")
         quantise_tiles("w2", 0, 2)
         quantise_tiles("w2", 2, 4)
-        round_weight("w3", slice(0, 4), 0, 40, "scalar")
-        round_weight("w3", slice(0, 4), 40, 128, "vector")
-        quantise_tiles("w3", 0, 4)
-        sum_chunk(0)
-        slope_chunk(0)
+        for c in range(4):
+            value_chunk(c)
+        round_weight("w3", slice(0, 4), 0, 44, "scalar")
+        round_weight("w3", slice(0, 2), 44, 128, "vector")
+        round_weight("w3", slice(2, 4), 44, 128, "vector")
+        quantise_tiles("w3", 0, 2)
+        for c in range(4):
+            sum_chunk(c)
+            slope_chunk(c)
         leaky_chunk(0)
-        sum_chunk(1)
-        slope_chunk(1)
-        leaky_chunk(1)
+        quantise_tiles("w3", 2, 4)
+        warm_up("dst", 2, "y0")
         quantise_hidden(0, 1)
         score_chunk(0)
-        sum_chunk(2)
-        slope_chunk(2)
+        leaky_chunk(1)
         leaky_chunk(2)
-        sum_chunk(3)
-        round_weight("w4", slice(0, 4), 0, 88, "scalar")
-        round_weight("w4", slice(0, 4), 88, 128, "vector")
         quantise_hidden(1, 1)
         score_chunk(1)
-        quantise_tiles("w4", 0, 4)
-        value_chunk(0)
+        leaky_chunk(3)
         quantise_hidden(2, 1)
         score_chunk(2)
-        value_chunk(1)
-        slope_chunk(3)
-        leaky_chunk(3)
-        exp_chunk(0)
-        exp_chunk(1)
-        exp_chunk(2)
-        message_chunk(0)
         quantise_hidden(3, 1)
         score_chunk(3)
-        exp_chunk(3)
-        value_chunk(2)
-        value_chunk(3)
-        message_chunk(1)
-        message_chunk(2)
-        message_chunk(3)
+        for c in range(4):
+            exp_chunk(c)
+            message_chunk(c)
         round_message(0, "scalar", 0, 128)
-        round_message(1, "vector", 0, 128)
-        round_message(2, "scalar", 0, 128)
+        round_message(1, "scalar", 0, 128)
+        round_message(2, "vector", 0, 128)
         quantise_message(0, 2)
         store_words(0, 2)
         round_message(3, "vector", 48, 128)

@@ -54,11 +54,14 @@ def tile_picked_zgatt_exp_po_kernel(
         nc.scalar.activation(warm[:, 1:2], warm[:, 0:1], ACT.Exp)
 
         raw = {}
-        for name, w, cuts in (("w1", w1, (0, 128)), ("w4", w4, (0, 128)), ("w2", w2, (0, 128)), ("w3", w3, (0, 128))):
+        for name, w, cuts in (("w1", w1, (0, 128)), ("w2", w2, (0, 128)), ("w4", w4, (0, 128)), ("w3", w3, (0, 128))):
             raw[name] = []
             rows = w.rearrange("(p j) c -> p j c", j=PACK)
             for first, last in zip(cuts, cuts[1:]):
-                tile = keep.tile([P, PACK, PACK * (last - first)], F32, name=f"raw_{name}_{first}", tag=f"raw_{name}_{first}")
+                if name == "w3":
+                    tile = reuse.tile([P, PACK, PACK * (last - first)], F32, name="raw_w3", offset=0, align_bytes=64)
+                else:
+                    tile = keep.tile([P, PACK, PACK * (last - first)], F32, name=f"raw_{name}_{first}", tag=f"raw_{name}_{first}")
                 nc.sync.dma_start(tile[:], rows[:, :, PACK * first : PACK * last])
                 raw[name].append((first, tile))
 
@@ -90,10 +93,7 @@ def tile_picked_zgatt_exp_po_kernel(
         grouped = {}
         weights = {}
         for name in ("w1", "w2", "w3", "w4"):
-            if name == "w3":
-                grouped[name] = reuse.tile([P, PACK, P, PACK], BF16, name="grouped_w3", offset=0, align_bytes=64)
-            else:
-                grouped[name] = keep.tile([P, PACK, P, PACK], BF16, name=f"grouped_{name}", align_bytes=64)
+            grouped[name] = keep.tile([P, PACK, P, PACK], BF16, name=f"grouped_{name}", align_bytes=64)
             words = keep.tile([P, PACK * P], U32, name=f"{name}_words", align_bytes=64)
             scales = keep.tile([P, PACK * P], U8, name=f"{name}_scales", align_bytes=64)
             weights[name] = (words, scales)
@@ -147,7 +147,10 @@ def tile_picked_zgatt_exp_po_kernel(
             product(sums[c], (("w1", picked["src"]), ("w2", picked["dst"])), cols)
 
         def slope_chunk(c):
-            rows = raw["w3"][0][1][:, :, c * CHUNK : (c + 1) * CHUNK]
+            rows = raw["w4"][0][1][:, :, c * CHUNK : (c + 1) * CHUNK]
+            if c == 2:
+                tile = reuse.tile([P, PACK, CHUNK], F32, name="sloped2", offset=2048, align_bytes=64)
+                rows = tile[:]
             if c == 3:
                 both = reuse.tile([P, 2, PACK, CHUNK // PACK, PACK], BF16, name="both", offset=0, align_bytes=64)
                 plain[c], sloped[c] = both[:, 0], both[:, 1]
@@ -199,6 +202,9 @@ def tile_picked_zgatt_exp_po_kernel(
         def round_message(c, engine, first, last):
             target = rounded[:, c * CHUNK + first : c * CHUNK + last, :].rearrange("p (g i) t -> p g t i", i=4)
             source = message[c][:, :, first:last].rearrange("p t (g i) -> p g t i", i=4)
+            if engine == "gpsimd":
+                target = rounded[:, c * CHUNK + first : c * CHUNK + last, :]
+                source = message[c][:, :, first:last].rearrange("p t n -> p n t")
             convert(target, source, engine)
 
         def quantise_message(first, count):
@@ -213,49 +219,51 @@ def tile_picked_zgatt_exp_po_kernel(
             cols = slice(first * CHUNK, (first + count) * CHUNK)
             nc.sync.dma_start(out_words_dram[:, cols], out_words[:, cols].bitcast(I32))
 
-        warm_up("dst", 2, "y3")
+        warm_up("dst", 3, "v3")
         round_weight("w1", slice(0, 4), 0, 128, "scalar")
         quantise_tiles("w1", 0, 4)
-        round_weight("w4", slice(0, 4), 0, 76, "scalar")
-        round_weight("w4", slice(0, 4), 76, 128, "vector")
-        quantise_tiles("w4", 0, 4)
-        round_weight("w2", slice(0, 2), 0, 128, "scalar")
-        round_weight("w2", slice(2, 4), 0, 128, "vector")
+        round_weight("w2", slice(0, 4), 0, 56, "scalar")
+        round_weight("w2", slice(0, 2), 56, 128, "vector")
+        round_weight("w2", slice(2, 4), 56, 128, "vector")
         quantise_tiles("w2", 0, 2)
         quantise_tiles("w2", 2, 4)
-        for c in range(4):
-            value_chunk(c)
-        round_weight("w3", slice(0, 4), 0, 44, "scalar")
-        round_weight("w3", slice(0, 2), 44, 128, "vector")
-        round_weight("w3", slice(2, 4), 44, 128, "vector")
-        quantise_tiles("w3", 0, 2)
+        round_weight("w4", slice(0, 4), 0, 40, "scalar")
+        round_weight("w4", slice(0, 4), 40, 128, "vector")
+        quantise_tiles("w4", 0, 4)
         for c in range(4):
             sum_chunk(c)
+        for c in range(4):
+            value_chunk(c)
+        for c in range(2):
             slope_chunk(c)
-        leaky_chunk(0)
-        quantise_tiles("w3", 2, 4)
-        warm_up("dst", 2, "y0")
+            leaky_chunk(c)
+        round_weight("w3", slice(0, 4), 0, 72, "scalar")
+        round_weight("w3", slice(0, 2), 72, 128, "vector")
+        round_weight("w3", slice(2, 4), 72, 128, "vector")
         quantise_hidden(0, 1)
+        quantise_tiles("w3", 0, 2)
+        quantise_tiles("w3", 2, 4)
         score_chunk(0)
-        leaky_chunk(1)
+        slope_chunk(2)
+        slope_chunk(3)
         leaky_chunk(2)
         quantise_hidden(1, 1)
         score_chunk(1)
-        leaky_chunk(3)
         quantise_hidden(2, 1)
         score_chunk(2)
+        leaky_chunk(3)
         quantise_hidden(3, 1)
         score_chunk(3)
         for c in range(4):
             exp_chunk(c)
             message_chunk(c)
-        round_message(0, "scalar", 0, 128)
+        round_message(0, "gpsimd", 0, 128)
         round_message(1, "scalar", 0, 128)
-        round_message(2, "vector", 0, 128)
+        round_message(2, "scalar", 0, 128)
         quantise_message(0, 2)
         store_words(0, 2)
-        round_message(3, "vector", 48, 128)
-        round_message(3, "scalar", 0, 48)
+        round_message(3, "vector", 32, 128)
+        round_message(3, "scalar", 0, 32)
         quantise_message(2, 1)
         quantise_message(3, 1)
         store_words(2, 2)

@@ -58,8 +58,8 @@ def tile_picked_zgatt_exp_po_kernel(
             raw[name] = []
             rows = w.rearrange("(p j) c -> p j c", j=PACK)
             for first, last in zip(cuts, cuts[1:]):
-                if name == "w3":
-                    tile = reuse.tile([P, PACK, PACK * (last - first)], F32, name="raw_w3", offset=0, align_bytes=64)
+                if name == "w4":
+                    tile = reuse.tile([P, PACK, PACK * (last - first)], F32, name="raw_w4", offset=0, align_bytes=64)
                 else:
                     tile = keep.tile([P, PACK, PACK * (last - first)], F32, name=f"raw_{name}_{first}", tag=f"raw_{name}_{first}")
                 nc.sync.dma_start(tile[:], rows[:, :, PACK * first : PACK * last])
@@ -149,8 +149,7 @@ def tile_picked_zgatt_exp_po_kernel(
         def slope_chunk(c):
             rows = raw["w4"][0][1][:, :, c * CHUNK : (c + 1) * CHUNK]
             if c == 2:
-                tile = reuse.tile([P, PACK, CHUNK], F32, name="sloped2", offset=2048, align_bytes=64)
-                rows = tile[:]
+                rows = raw["w3"][0][1][:, :, 0:CHUNK]
             if c == 3:
                 both = reuse.tile([P, 2, PACK, CHUNK // PACK, PACK], BF16, name="both", offset=0, align_bytes=64)
                 plain[c], sloped[c] = both[:, 0], both[:, 1]
@@ -219,16 +218,16 @@ def tile_picked_zgatt_exp_po_kernel(
             cols = slice(first * CHUNK, (first + count) * CHUNK)
             nc.sync.dma_start(out_words_dram[:, cols], out_words[:, cols].bitcast(I32))
 
-        warm_up("dst", 3, "v3")
+        warm_up("src", 4, "v3")
         round_weight("w1", slice(0, 4), 0, 128, "scalar")
         quantise_tiles("w1", 0, 4)
-        round_weight("w2", slice(0, 4), 0, 56, "scalar")
-        round_weight("w2", slice(0, 2), 56, 128, "vector")
-        round_weight("w2", slice(2, 4), 56, 128, "vector")
+        round_weight("w2", slice(0, 4), 0, 64, "scalar")
+        round_weight("w2", slice(0, 2), 64, 128, "vector")
+        round_weight("w2", slice(2, 4), 64, 128, "vector")
         quantise_tiles("w2", 0, 2)
         quantise_tiles("w2", 2, 4)
-        round_weight("w4", slice(0, 4), 0, 40, "scalar")
-        round_weight("w4", slice(0, 4), 40, 128, "vector")
+        round_weight("w4", slice(0, 4), 0, 48, "scalar")
+        round_weight("w4", slice(0, 4), 48, 128, "vector")
         quantise_tiles("w4", 0, 4)
         for c in range(4):
             sum_chunk(c)
@@ -237,7 +236,8 @@ def tile_picked_zgatt_exp_po_kernel(
         for c in range(2):
             slope_chunk(c)
             leaky_chunk(c)
-        round_weight("w3", slice(0, 4), 0, 72, "scalar")
+        round_weight("w3", slice(0, 4), 0, 48, "scalar")
+        round_weight("w3", slice(0, 4), 48, 72, "scalar")
         round_weight("w3", slice(0, 2), 72, 128, "vector")
         round_weight("w3", slice(2, 4), 72, 128, "vector")
         quantise_hidden(0, 1)

@@ -18,11 +18,19 @@ ACT = mybir.ActivationFunctionType
 P = 128
 PACK = 4
 CHUNK = 128
+CHUNKS = S // CHUNK
+LAST = CHUNKS - 1
+QUADRANTS = 4
 SLOPE = 0.2
 WARM_PASSES = 4
-SUM_BANK = ("y0", "y1", "y2", "y3")
-SCORE_BANK = ("y0", "y1", "y2", "y3")
-VALUE_BANK = ("v0", "v1", "v2", "v3")
+ALL_TILES = slice(0, PACK)
+TILE_PAIRS = (slice(0, 2), slice(2, 4))
+SCALAR_W2 = 64
+SCALAR_W4 = 48
+SCALAR_W3 = 64
+SCALAR_W3_FIRST = 48
+GPSIMD_W3 = 24
+SCALAR_LAST_EDGES = 64
 
 
 def tile_picked_zgatt_exp_po_kernel(
@@ -40,30 +48,26 @@ def tile_picked_zgatt_exp_po_kernel(
         dst_list = keep.tile([P, S // 16], U16, name="dst_list")
 
         nc.vector.memset(table_scales[:].bitcast(I32), 0)
-        warm = keep.tile([P, 2], F32, name="warm")
-        nc.vector.memset(warm[:, 0:1], 0.0)
+        exp_probe = keep.tile([P, 2], F32, name="exp_probe")
+        nc.vector.memset(exp_probe[:, 0:1], 0.0)
 
         nc.sync.dma_start(table_words[:], x_words[0].rearrange("p c r -> p (c r)").bitcast(I32))
         nc.sync.dma_start(src_list[:], offs)
         nc.sync.dma_start(dst_list[:], dst)
-        for q in range(4):
+        for q in range(QUADRANTS):
             nc.scalar.dma_start(
                 table_scales[32 * q : 32 * q + 4, :].bitcast(I32),
                 x_scales[0][4 * q : 4 * q + 4, :].bitcast(I32),
             )
-        nc.scalar.activation(warm[:, 1:2], warm[:, 0:1], ACT.Exp)
+        nc.scalar.activation(exp_probe[:, 1:2], exp_probe[:, 0:1], ACT.Exp)
 
         raw = {}
-        for name, w, cuts in (("w1", w1, (0, 128)), ("w2", w2, (0, 128)), ("w4", w4, (0, 128)), ("w3", w3, (0, 128))):
-            raw[name] = []
-            rows = w.rearrange("(p j) c -> p j c", j=PACK)
-            for first, last in zip(cuts, cuts[1:]):
-                if name == "w4":
-                    tile = reuse.tile([P, PACK, PACK * (last - first)], F32, name="raw_w4", offset=0, align_bytes=64)
-                else:
-                    tile = keep.tile([P, PACK, PACK * (last - first)], F32, name=f"raw_{name}_{first}", tag=f"raw_{name}_{first}")
-                nc.sync.dma_start(tile[:], rows[:, :, PACK * first : PACK * last])
-                raw[name].append((first, tile))
+        for name, w in (("w1", w1), ("w2", w2), ("w4", w4), ("w3", w3)):
+            if name == "w4":
+                raw[name] = reuse.tile([P, PACK, N], F32, name="raw_w4", offset=0, align_bytes=64)
+            else:
+                raw[name] = keep.tile([P, PACK, N], F32, name=f"raw_{name}")
+            nc.sync.dma_start(raw[name][:], w.rearrange("(p j) c -> p j c", j=PACK))
 
         picked = {}
         for name in ("src", "dst"):
@@ -75,25 +79,11 @@ def tile_picked_zgatt_exp_po_kernel(
         for name, entries in (("src", src_list), ("dst", dst_list)):
             nc.vector.tensor_copy(picked[name][1][:], table_scales[:].indirect(entries[:]))
 
-
-        def warm_up(name, passes, bank):
-            words, scales = picked[name]
-            idle_bank = psum.tile([P, S], F32, name=f"idle_{bank}", tag=bank)
-            for n in range(passes):
-                nc.tensor.matmul_mx(
-                    out=idle_bank[:],
-                    lhsT=words[:, 0:P].bitcast(FP8X4),
-                    lhsT_scale=scales[:, 0:P],
-                    rhs=words[:].bitcast(FP8X4),
-                    rhs_scale=scales[:],
-                    start=True,
-                    stop=True,
-                )
-
         grouped = {}
         weights = {}
-        for name in ("w1", "w2", "w3", "w4"):
-            grouped[name] = keep.tile([P, PACK, P, PACK], BF16, name=f"grouped_{name}", align_bytes=64)
+        for name in ("w1", "w2", "w4", "w3"):
+            place = "grouped_w4" if name == "w3" else f"grouped_{name}"
+            grouped[name] = keep.tile([P, PACK, P, PACK], BF16, name=f"grouped_{name}", tag=place, align_bytes=64)
             words = keep.tile([P, PACK * P], U32, name=f"{name}_words", align_bytes=64)
             scales = keep.tile([P, PACK * P], U8, name=f"{name}_scales", align_bytes=64)
             weights[name] = (words, scales)
@@ -107,31 +97,38 @@ def tile_picked_zgatt_exp_po_kernel(
                 nc.scalar.copy(target, source)
 
         def round_weight(name, tiles, first, last, engine):
-            start, tile = [piece for piece in raw[name] if piece[0] <= first][-1]
-            target = grouped[name][:, tiles, first:last, :].rearrange("p t m j -> p m j t")
-            source = tile[:].rearrange("p j (m t) -> p t m j", t=PACK)[:, tiles, first - start : last - start, :]
-            convert(target, source.rearrange("p t m j -> p m j t"), engine)
+            walk = "p t m j -> p m t j" if engine == "gpsimd" else "p t m j -> p m j t"
+            target = grouped[name][:, tiles, first:last, :]
+            source = raw[name][:].rearrange("p j (m t) -> p t m j", t=PACK)[:, tiles, first:last, :]
+            convert(target.rearrange(walk), source.rearrange(walk), engine)
 
-        def quantise_tiles(name, first, last):
+        def round_rest_by_pairs(name, first):
+            for pair in TILE_PAIRS:
+                round_weight(name, pair, first, P, "vector")
+
+        def quantise_weight(name, tiles):
             words, scales = weights[name]
             flat = grouped[name][:].rearrange("p t m j -> p (t m j)")
             nc.vector.quantize_mx(
-                out=words[:, first * P : last * P].bitcast(FP8X4),
-                scales=scales[:, first * P : last * P],
-                in_=flat[:, PACK * first * P : PACK * last * P],
+                out=words[:, tiles.start * P : tiles.stop * P].bitcast(FP8X4),
+                scales=scales[:, tiles.start * P : tiles.stop * P],
+                in_=flat[:, PACK * tiles.start * P : PACK * tiles.stop * P],
             )
 
-        def product(bank, terms, cols):
+        def edges(c):
+            return slice(c * CHUNK, (c + 1) * CHUNK)
+
+        def product(bank, terms, c):
             for t in range(PACK):
-                tile_cols = slice(t * P, (t + 1) * P)
+                places = slice(t * P, (t + 1) * P)
                 for n, (name, (words, scales)) in enumerate(terms):
                     w_words, w_scales = weights[name]
                     nc.tensor.matmul_mx(
                         out=bank[:, t, :],
-                        lhsT=w_words[:, tile_cols].bitcast(FP8X4),
-                        lhsT_scale=w_scales[:, tile_cols],
-                        rhs=words[:, cols].bitcast(FP8X4),
-                        rhs_scale=scales[:, cols],
+                        lhsT=w_words[:, places].bitcast(FP8X4),
+                        lhsT_scale=w_scales[:, places],
+                        rhs=words[:, edges(c)].bitcast(FP8X4),
+                        rhs_scale=scales[:, edges(c)],
                         start=(n == 0),
                         stop=(n == len(terms) - 1),
                     )
@@ -142,34 +139,32 @@ def tile_picked_zgatt_exp_po_kernel(
         sums, plain, sloped, scores, values, exps, message = {}, {}, {}, {}, {}, {}, {}
 
         def sum_chunk(c):
-            cols = slice(c * CHUNK, (c + 1) * CHUNK)
-            sums[c] = psum.tile([P, PACK, CHUNK], F32, name=f"y{c}", tag=SUM_BANK[c])
-            product(sums[c], (("w1", picked["src"]), ("w2", picked["dst"])), cols)
+            sums[c] = psum.tile([P, PACK, CHUNK], F32, name=f"y{c}", tag=f"y{c}")
+            product(sums[c], (("w1", picked["src"]), ("w2", picked["dst"])), c)
 
-        def slope_chunk(c):
-            rows = raw["w4"][0][1][:, :, c * CHUNK : (c + 1) * CHUNK]
-            if c == 2:
-                rows = raw["w3"][0][1][:, :, 0:CHUNK]
-            if c == 3:
-                both = reuse.tile([P, 2, PACK, CHUNK // PACK, PACK], BF16, name="both", offset=0, align_bytes=64)
-                plain[c], sloped[c] = both[:, 0], both[:, 1]
-                nc.scalar.copy(plain[c], sums[c][:].rearrange("p t (r n) -> p r n t", r=PACK))
-            else:
-                plain[c] = sums[c][:].rearrange("p t (r n) -> p r n t", r=PACK)
-                sloped[c] = rows.rearrange("p r (n t) -> p r n t", t=PACK)
-            nc.scalar.activation(sloped[c], sums[c][:].rearrange("p t (r n) -> p r n t", r=PACK), ACT.Copy, scale=SLOPE)
+        def interleaved(c):
+            return sums[c][:].rearrange("p t (r n) -> p r n t", r=PACK)
+
+        def slope_chunk(c, dead):
+            plain[c] = interleaved(c)
+            sloped[c] = dead.rearrange("p r (n t) -> p r n t", t=PACK)
+            nc.scalar.activation(sloped[c], interleaved(c), ACT.Copy, scale=SLOPE)
+
+        def slope_last_chunk():
+            both = reuse.tile([P, 2, PACK, CHUNK // PACK, PACK], BF16, name="both", offset=0, align_bytes=64)
+            plain[LAST], sloped[LAST] = both[:, 0], both[:, 1]
+            nc.scalar.copy(plain[LAST], interleaved(LAST))
+            nc.scalar.activation(sloped[LAST], interleaved(LAST), ACT.Copy, scale=SLOPE)
 
         def leaky_chunk(c):
-            cols = slice(c * CHUNK, (c + 1) * CHUNK)
-            target = hidden[:, cols, :].rearrange("p (r n) t -> p r n t", r=PACK)
+            target = hidden[:, edges(c), :].rearrange("p (r n) t -> p r n t", r=PACK)
             nc.vector.tensor_tensor(target, plain[c], sloped[c], ALU.max)
 
-        def quantise_hidden(first, count):
-            cols = slice(first * CHUNK, (first + count) * CHUNK)
+        def quantise_hidden(c):
             nc.vector.quantize_mx(
-                out=h_words[:, cols].bitcast(FP8X4),
-                scales=h_scales[:, cols],
-                in_=hidden[:, cols, :].rearrange("p n t -> p (n t)"),
+                out=h_words[:, edges(c)].bitcast(FP8X4),
+                scales=h_scales[:, edges(c)],
+                in_=hidden[:, edges(c), :].rearrange("p n t -> p (n t)"),
             )
 
         out_rows = out_0.rearrange("(p t) n -> p t n", t=PACK)
@@ -179,32 +174,33 @@ def tile_picked_zgatt_exp_po_kernel(
         rounded = keep.tile([P, S, PACK], BF16, name="rounded", align_bytes=64)
 
         def score_chunk(c):
-            cols = slice(c * CHUNK, (c + 1) * CHUNK)
-            scores[c] = psum.tile([P, PACK, CHUNK], F32, name=f"score{c}", tag=SCORE_BANK[c])
-            product(scores[c], (("w3", (h_words, h_scales)),), cols)
+            scores[c] = psum.tile([P, PACK, CHUNK], F32, name=f"score{c}", tag=f"y{c}")
+            product(scores[c], (("w3", (h_words, h_scales)),), c)
 
         def exp_chunk(c):
             exps[c] = keep.tile([P, PACK, CHUNK], F32, name=f"e{c}")
             nc.scalar.activation(exps[c][:], scores[c][:], ACT.Exp)
 
         def value_chunk(c):
-            cols = slice(c * CHUNK, (c + 1) * CHUNK)
-            values[c] = psum.tile([P, PACK, CHUNK], F32, name=f"value{c}", tag=VALUE_BANK[c])
-            product(values[c], (("w4", picked["src"]),), cols)
+            values[c] = psum.tile([P, PACK, CHUNK], F32, name=f"value{c}", tag=f"v{c}")
+            product(values[c], (("w4", picked["src"]),), c)
 
         def message_chunk(c):
-            cols = slice(c * CHUNK, (c + 1) * CHUNK)
             message[c] = keep.tile([P, PACK, CHUNK], F32, name=f"result{c}")
-            nc.vector.tensor_tensor(message[c][:], values[c][:], exps[c][:], ALU.mult)
-            nc.sync.dma_start(out_rows[:, :, cols], message[c][:])
+            cuts = (0, SCALAR_LAST_EDGES, CHUNK) if c == LAST else (0, CHUNK)
+            for first, last in zip(cuts, cuts[1:]):
+                part = slice(first, last)
+                nc.vector.tensor_tensor(message[c][:, :, part], values[c][:, :, part], exps[c][:, :, part], ALU.mult)
+            nc.sync.dma_start(out_rows[:, :, edges(c)], message[c][:])
 
         def round_message(c, engine, first, last):
-            target = rounded[:, c * CHUNK + first : c * CHUNK + last, :].rearrange("p (g i) t -> p g t i", i=4)
-            source = message[c][:, :, first:last].rearrange("p t (g i) -> p g t i", i=4)
+            target = rounded[:, c * CHUNK + first : c * CHUNK + last, :]
+            source = message[c][:, :, first:last]
             if engine == "gpsimd":
-                target = rounded[:, c * CHUNK + first : c * CHUNK + last, :]
-                source = message[c][:, :, first:last].rearrange("p t n -> p n t")
-            convert(target, source, engine)
+                convert(target, source.rearrange("p t n -> p n t"), engine)
+            else:
+                target = target.rearrange("p (g i) t -> p g t i", i=4)
+                convert(target, source.rearrange("p t (g i) -> p g t i", i=4), engine)
 
         def quantise_message(first, count):
             cols = slice(first * CHUNK, (first + count) * CHUNK)
@@ -218,57 +214,70 @@ def tile_picked_zgatt_exp_po_kernel(
             cols = slice(first * CHUNK, (first + count) * CHUNK)
             nc.sync.dma_start(out_words_dram[:, cols], out_words[:, cols].bitcast(I32))
 
-        warm_up("src", 4, "v3")
-        round_weight("w1", slice(0, 4), 0, 128, "scalar")
-        quantise_tiles("w1", 0, 4)
-        round_weight("w2", slice(0, 4), 0, 64, "scalar")
-        round_weight("w2", slice(0, 2), 64, 128, "vector")
-        round_weight("w2", slice(2, 4), 64, 128, "vector")
-        quantise_tiles("w2", 0, 2)
-        quantise_tiles("w2", 2, 4)
-        round_weight("w4", slice(0, 4), 0, 48, "scalar")
-        round_weight("w4", slice(0, 4), 48, 128, "vector")
-        quantise_tiles("w4", 0, 4)
-        for c in range(4):
+        src_words, src_scales = picked["src"]
+        idle_bank = psum.tile([P, S], F32, name="idle_bank", tag=f"v{LAST}")
+        for n in range(WARM_PASSES):
+            nc.tensor.matmul_mx(
+                out=idle_bank[:],
+                lhsT=src_words[:, 0:P].bitcast(FP8X4),
+                lhsT_scale=src_scales[:, 0:P],
+                rhs=src_words[:].bitcast(FP8X4),
+                rhs_scale=src_scales[:],
+                start=True,
+                stop=True,
+            )
+
+        round_weight("w1", ALL_TILES, 0, P, "scalar")
+        quantise_weight("w1", ALL_TILES)
+        round_weight("w2", ALL_TILES, 0, SCALAR_W2, "scalar")
+        round_rest_by_pairs("w2", SCALAR_W2)
+        for pair in TILE_PAIRS:
+            quantise_weight("w2", pair)
+        round_weight("w4", ALL_TILES, 0, SCALAR_W4, "scalar")
+        round_rest_by_pairs("w4", SCALAR_W4)
+        for pair in TILE_PAIRS:
+            quantise_weight("w4", pair)
+        for c in range(CHUNKS):
             sum_chunk(c)
-        for c in range(4):
+        for c in range(CHUNKS):
             value_chunk(c)
+
         for c in range(2):
-            slope_chunk(c)
+            slope_chunk(c, raw["w4"][:, :, edges(c)])
             leaky_chunk(c)
-        round_weight("w3", slice(0, 4), 0, 48, "scalar")
-        round_weight("w3", slice(0, 4), 48, 72, "scalar")
-        round_weight("w3", slice(0, 2), 72, 128, "vector")
-        round_weight("w3", slice(2, 4), 72, 128, "vector")
-        quantise_hidden(0, 1)
-        quantise_tiles("w3", 0, 2)
-        quantise_tiles("w3", 2, 4)
+        round_weight("w3", ALL_TILES, 0, SCALAR_W3_FIRST, "scalar")
+        round_weight("w3", ALL_TILES, SCALAR_W3_FIRST, SCALAR_W3, "scalar")
+        round_weight("w3", ALL_TILES, SCALAR_W3, SCALAR_W3 + GPSIMD_W3, "gpsimd")
+        round_rest_by_pairs("w3", SCALAR_W3 + GPSIMD_W3)
+        quantise_hidden(0)
+        for pair in TILE_PAIRS:
+            quantise_weight("w3", pair)
         score_chunk(0)
-        slope_chunk(2)
-        slope_chunk(3)
+        slope_chunk(2, raw["w3"][:, :, 0:CHUNK])
+        slope_last_chunk()
         leaky_chunk(2)
-        quantise_hidden(1, 1)
-        score_chunk(1)
-        quantise_hidden(2, 1)
-        score_chunk(2)
-        leaky_chunk(3)
-        quantise_hidden(3, 1)
-        score_chunk(3)
-        for c in range(4):
+        for c in (1, 2):
+            quantise_hidden(c)
+            score_chunk(c)
+        leaky_chunk(LAST)
+        quantise_hidden(LAST)
+        score_chunk(LAST)
+
+        for c in range(CHUNKS):
             exp_chunk(c)
             message_chunk(c)
-        round_message(0, "gpsimd", 0, 128)
-        round_message(1, "scalar", 0, 128)
-        round_message(2, "scalar", 0, 128)
+        round_message(0, "gpsimd", 0, CHUNK)
+        round_message(1, "scalar", 0, CHUNK)
+        round_message(2, "scalar", 0, CHUNK)
         quantise_message(0, 2)
         store_words(0, 2)
-        round_message(3, "vector", 32, 128)
-        round_message(3, "scalar", 0, 32)
+        round_message(LAST, "vector", SCALAR_LAST_EDGES, CHUNK)
+        round_message(LAST, "scalar", 0, SCALAR_LAST_EDGES)
         quantise_message(2, 1)
-        quantise_message(3, 1)
+        quantise_message(LAST, 1)
         store_words(2, 2)
 
-        for q in range(4):
+        for q in range(QUADRANTS):
             queue = nc.scalar if q % 2 else nc.sync
             queue.dma_start(
                 out_2[0][4 * q : 4 * q + 4, :].bitcast(I32),

@@ -22,7 +22,7 @@ CHUNKS = S // CHUNK
 LAST = CHUNKS - 1
 QUADRANTS = 4
 SLOPE = 0.2
-WARM_PASSES = 4
+WARM_WIDTHS = (512, 256)
 ALL_TILES = slice(0, PACK)
 TILE_PAIRS = (slice(0, 2), slice(2, 4))
 SCALAR_W2 = 64
@@ -133,14 +133,29 @@ def tile_picked_zgatt_exp_po_kernel(
                         stop=(n == len(terms) - 1),
                     )
 
+        def add_term(c, name, operand, opens):
+            w_words, w_scales = weights[name]
+            words, scales = picked[operand]
+            for t in range(PACK):
+                places = slice(t * P, (t + 1) * P)
+                nc.tensor.matmul_mx(
+                    out=sums[c][:, t, :],
+                    lhsT=w_words[:, places].bitcast(FP8X4),
+                    lhsT_scale=w_scales[:, places],
+                    rhs=words[:, edges(c)].bitcast(FP8X4),
+                    rhs_scale=scales[:, edges(c)],
+                    start=(opens and t == 0),
+                    stop=(not opens and t == PACK - 1),
+                )
+
         hidden = keep.tile([P, S, PACK], BF16, name="hidden", align_bytes=64)
         h_words = keep.tile([P, S], U32, name="h_words", align_bytes=64)
         h_scales = keep.tile([P, S], U8, name="h_scales", align_bytes=64)
         sums, plain, sloped, scores, values, exps, message = {}, {}, {}, {}, {}, {}, {}
 
-        def sum_chunk(c):
+        def open_sums(c, name, operand):
             sums[c] = psum.tile([P, PACK, CHUNK], F32, name=f"y{c}", tag=f"y{c}")
-            product(sums[c], (("w1", picked["src"]), ("w2", picked["dst"])), c)
+            add_term(c, name, operand, True)
 
         def interleaved(c):
             return sums[c][:].rearrange("p t (r n) -> p r n t", r=PACK)
@@ -216,19 +231,21 @@ def tile_picked_zgatt_exp_po_kernel(
 
         src_words, src_scales = picked["src"]
         idle_bank = psum.tile([P, S], F32, name="idle_bank", tag=f"v{LAST}")
-        for n in range(WARM_PASSES):
+        for width in WARM_WIDTHS:
             nc.tensor.matmul_mx(
-                out=idle_bank[:],
+                out=idle_bank[:, 0:width],
                 lhsT=src_words[:, 0:P].bitcast(FP8X4),
                 lhsT_scale=src_scales[:, 0:P],
-                rhs=src_words[:].bitcast(FP8X4),
-                rhs_scale=src_scales[:],
+                rhs=src_words[:, 0:width].bitcast(FP8X4),
+                rhs_scale=src_scales[:, 0:width],
                 start=True,
                 stop=True,
             )
 
         round_weight("w1", ALL_TILES, 0, P, "scalar")
         quantise_weight("w1", ALL_TILES)
+        for c in range(2):
+            open_sums(c, "w1", "src")
         round_weight("w2", ALL_TILES, 0, SCALAR_W2, "scalar")
         round_rest_by_pairs("w2", SCALAR_W2)
         for pair in TILE_PAIRS:
@@ -237,8 +254,11 @@ def tile_picked_zgatt_exp_po_kernel(
         round_rest_by_pairs("w4", SCALAR_W4)
         for pair in TILE_PAIRS:
             quantise_weight("w4", pair)
-        for c in range(CHUNKS):
-            sum_chunk(c)
+        for c in range(2):
+            add_term(c, "w2", "dst", False)
+        for c in range(2, CHUNKS):
+            open_sums(c, "w2", "dst")
+            add_term(c, "w1", "src", False)
         for c in range(CHUNKS):
             value_chunk(c)
 

@@ -22,7 +22,6 @@ CHUNKS = S // CHUNK
 LAST = CHUNKS - 1
 QUADRANTS = 4
 SLOPE = 0.2
-WARM_WIDTHS = (512, 256)
 ALL_TILES = slice(0, PACK)
 TILE_PAIRS = (slice(0, 2), slice(2, 4))
 SCALAR_W2 = 64
@@ -154,7 +153,7 @@ def tile_picked_zgatt_exp_po_kernel(
         sums, plain, sloped, scores, values, exps, message = {}, {}, {}, {}, {}, {}, {}
 
         def open_sums(c, name, operand):
-            sums[c] = psum.tile([P, PACK, CHUNK], F32, name=f"y{c}", tag=f"y{c}")
+            sums[c] = psum.tile([P, PACK, CHUNK], F32, name=f"y{c}", tag=f"y{c % LAST}")
             add_term(c, name, operand, True)
 
         def interleaved(c):
@@ -189,7 +188,7 @@ def tile_picked_zgatt_exp_po_kernel(
         rounded = keep.tile([P, S, PACK], BF16, name="rounded", align_bytes=64)
 
         def score_chunk(c):
-            scores[c] = psum.tile([P, PACK, CHUNK], F32, name=f"score{c}", tag=f"y{c}")
+            scores[c] = psum.tile([P, PACK, CHUNK], F32, name=f"score{c}", tag=f"y{LAST if c == 0 else c % LAST}")
             product(scores[c], (("w3", (h_words, h_scales)),), c)
 
         def exp_chunk(c):
@@ -229,19 +228,6 @@ def tile_picked_zgatt_exp_po_kernel(
             cols = slice(first * CHUNK, (first + count) * CHUNK)
             nc.sync.dma_start(out_words_dram[:, cols], out_words[:, cols].bitcast(I32))
 
-        src_words, src_scales = picked["src"]
-        idle_bank = psum.tile([P, S], F32, name="idle_bank", tag=f"v{LAST}")
-        for width in WARM_WIDTHS:
-            nc.tensor.matmul_mx(
-                out=idle_bank[:, 0:width],
-                lhsT=src_words[:, 0:P].bitcast(FP8X4),
-                lhsT_scale=src_scales[:, 0:P],
-                rhs=src_words[:, 0:width].bitcast(FP8X4),
-                rhs_scale=src_scales[:, 0:width],
-                start=True,
-                stop=True,
-            )
-
         round_weight("w1", ALL_TILES, 0, P, "scalar")
         quantise_weight("w1", ALL_TILES)
         for c in range(2):
@@ -256,15 +242,18 @@ def tile_picked_zgatt_exp_po_kernel(
             quantise_weight("w4", pair)
         for c in range(2):
             add_term(c, "w2", "dst", False)
-        for c in range(2, CHUNKS):
-            open_sums(c, "w2", "dst")
-            add_term(c, "w1", "src", False)
-        for c in range(CHUNKS):
+        open_sums(2, "w2", "dst")
+        add_term(2, "w1", "src", False)
+        for c in range(2):
             value_chunk(c)
 
         for c in range(2):
             slope_chunk(c, raw["w4"][:, :, edges(c)])
             leaky_chunk(c)
+        open_sums(LAST, "w2", "dst")
+        add_term(LAST, "w1", "src", False)
+        for c in range(2, CHUNKS):
+            value_chunk(c)
         round_weight("w3", ALL_TILES, 0, SCALAR_W3_FIRST, "scalar")
         round_weight("w3", ALL_TILES, SCALAR_W3_FIRST, SCALAR_W3, "scalar")
         round_weight("w3", ALL_TILES, SCALAR_W3, SCALAR_W3 + GPSIMD_W3, "gpsimd")

@@ -96,10 +96,14 @@ def tile_picked_zgatt_exp_po_kernel(
                 nc.scalar.copy(target, source)
 
         def round_weight(name, tiles, first, last, engine):
-            walk = "p t m j -> p m t j" if engine == "gpsimd" else "p t m j -> p m j t"
             target = grouped[name][:, tiles, first:last, :]
             source = raw[name][:].rearrange("p j (m t) -> p t m j", t=PACK)[:, tiles, first:last, :]
-            convert(target.rearrange(walk), source.rearrange(walk), engine)
+            if engine == "scalar":
+                walk = "p t (g i) j -> p g j i t"
+                convert(target.rearrange(walk, i=2), source.rearrange(walk, i=2), engine)
+            else:
+                walk = "p t m j -> p m t j" if engine == "gpsimd" else "p t m j -> p m j t"
+                convert(target.rearrange(walk), source.rearrange(walk), engine)
 
         def round_rest_by_pairs(name, first):
             for pair in TILE_PAIRS:
@@ -213,8 +217,9 @@ def tile_picked_zgatt_exp_po_kernel(
             if engine == "gpsimd":
                 convert(target, source.rearrange("p t n -> p n t"), engine)
             else:
-                target = target.rearrange("p (g i) t -> p g t i", i=4)
-                convert(target, source.rearrange("p t (g i) -> p g t i", i=4), engine)
+                run = 8 if engine == "scalar" else 4
+                target = target.rearrange("p (g i) t -> p g t i", i=run)
+                convert(target, source.rearrange("p t (g i) -> p g t i", i=run), engine)
 
         def quantise_message(first, count):
             cols = slice(first * CHUNK, (first + count) * CHUNK)

@@ -30,6 +30,8 @@ SCALAR_W3 = 64
 SCALAR_W3_FIRST = 48
 GPSIMD_W3 = 24
 SCALAR_LAST_EDGES = 64
+WARM_UP_PASSES = 4
+WARM_UP_ROWS = 32
 
 
 def tile_picked_zgatt_exp_po_kernel(
@@ -232,6 +234,20 @@ def tile_picked_zgatt_exp_po_kernel(
         def store_words(first, count):
             cols = slice(first * CHUNK, (first + count) * CHUNK)
             nc.sync.dma_start(out_words_dram[:, cols], out_words[:, cols].bitcast(I32))
+
+        idle = psum.tile([WARM_UP_ROWS, S], F32, name="idle", tag=f"y{LAST}")
+        src_words, src_scales = picked["src"]
+        for n in range(WARM_UP_PASSES):
+            places = slice(n * P, n * P + WARM_UP_ROWS)
+            nc.tensor.matmul_mx(
+                out=idle[:],
+                lhsT=src_words[:, places].bitcast(FP8X4),
+                lhsT_scale=src_scales[:, places],
+                rhs=src_words[:].bitcast(FP8X4),
+                rhs_scale=src_scales[:],
+                start=True,
+                stop=True,
+            )
 
         round_weight("w1", ALL_TILES, 0, P, "scalar")
         quantise_weight("w1", ALL_TILES)

from contextlib import ExitStack

import concourse.mybir as mybir

K, T, S, H, N = 512, 1024, 512, 512, 512
FLOPS = 2 * S * (2 * K * H + H * N + K * N)

F32 = mybir.dt.float32
BF16 = mybir.dt.bfloat16
I32 = mybir.dt.int32
U32 = mybir.dt.uint32
U16 = mybir.dt.uint16
U8 = mybir.dt.uint8
FP8X4 = mybir.dt.float8_e4m3fn_x4
ALU = mybir.AluOpType
ACT = mybir.ActivationFunctionType

P = 128
PACK = 4
CHUNK = 128
CHUNKS = S // CHUNK
LAST = CHUNKS - 1
QUADRANTS = 4
SLOPE = 0.2
ALL_TILES = slice(0, PACK)
TILE_PAIRS = (slice(0, 2), slice(2, 4))
SCALAR_W2 = 64
SCALAR_W4 = 48
SCALAR_W3 = 64
SCALAR_W3_FIRST = 48
GPSIMD_W3 = 24
SCALAR_LAST_EDGES = 64
WARM_UP_PASSES = 4
WARM_UP_ROWS = 32


def tile_picked_zgatt_exp_po_kernel(
    tc, x_words, x_scales, w1, w2, w3, w4, offs, dst, out_0, out_1, out_2
):
    nc = tc.nc
    with ExitStack() as ctx:
        keep = ctx.enter_context(tc.tile_pool(name="keep", bufs=1))
        reuse = ctx.enter_context(tc.tile_pool(name="reuse", bufs=1))
        psum = ctx.enter_context(tc.psum_pool(name="psum", bufs=1))

        table_words = keep.tile([P, T], I32, name="table_words")
        table_scales = keep.tile([P, T], U8, name="table_scales")
        src_list = keep.tile([P, S // 16], U16, name="src_list")
        dst_list = keep.tile([P, S // 16], U16, name="dst_list")

        nc.vector.memset(table_scales[:].bitcast(I32), 0)
        exp_probe = keep.tile([P, 2], F32, name="exp_probe")
        nc.vector.memset(exp_probe[:, 0:1], 0.0)

        nc.sync.dma_start(table_words[:], x_words[0].rearrange("p c r -> p (c r)").bitcast(I32))
        nc.sync.dma_start(src_list[:], offs)
        nc.sync.dma_start(dst_list[:], dst)
        for q in range(QUADRANTS):
            nc.scalar.dma_start(
                table_scales[32 * q : 32 * q + 4, :].bitcast(I32),
                x_scales[0][4 * q : 4 * q + 4, :].bitcast(I32),
            )
        nc.scalar.activation(exp_probe[:, 1:2], exp_probe[:, 0:1], ACT.Exp)

        raw = {}
        for name, w in (("w1", w1), ("w2", w2), ("w4", w4), ("w3", w3)):
            if name == "w4":
                raw[name] = reuse.tile([P, PACK, N], F32, name="raw_w4", offset=0, align_bytes=64)
            else:
                raw[name] = keep.tile([P, PACK, N], F32, name=f"raw_{name}")
            nc.sync.dma_start(raw[name][:], w.rearrange("(p j) c -> p j c", j=PACK))

        picked = {}
        for name in ("src", "dst"):
            words = keep.tile([P, S], U32, name=f"{name}_words", align_bytes=64)
            scales = keep.tile([P, S], U8, name=f"{name}_scales", align_bytes=64)
            picked[name] = (words, scales)
        for name, entries in (("src", src_list), ("dst", dst_list)):
            nc.vector.tensor_copy(picked[name][0][:], table_words[:].bitcast(U32).indirect(entries[:]))
        for name, entries in (("src", src_list), ("dst", dst_list)):
            nc.vector.tensor_copy(picked[name][1][:], table_scales[:].indirect(entries[:]))

        grouped = {}
        weights = {}
        for name in ("w1", "w2", "w4", "w3"):
            place = "grouped_w4" if name == "w3" else f"grouped_{name}"
            grouped[name] = keep.tile([P, PACK, P, PACK], BF16, name=f"grouped_{name}", tag=place, align_bytes=64)
            words = keep.tile([P, PACK * P], U32, name=f"{name}_words", align_bytes=64)
            scales = keep.tile([P, PACK * P], U8, name=f"{name}_scales", align_bytes=64)
            weights[name] = (words, scales)

        def convert(target, source, engine):
            if engine == "vector":
                nc.vector.tensor_copy(target, source)
            elif engine == "gpsimd":
                nc.gpsimd.tensor_scalar(target, source, 1.0, 0.0, ALU.mult, ALU.add)
            else:
                nc.scalar.copy(target, source)

        def round_weight(name, tiles, first, last, engine):
            target = grouped[name][:, tiles, first:last, :]
            source = raw[name][:].rearrange("p j (m t) -> p t m j", t=PACK)[:, tiles, first:last, :]
            if engine == "scalar":
                walk = "p t (g i) j -> p g j i t"
                convert(target.rearrange(walk, i=2), source.rearrange(walk, i=2), engine)
            else:
                walk = "p t m j -> p m t j" if engine == "gpsimd" else "p t m j -> p m j t"
                convert(target.rearrange(walk), source.rearrange(walk), engine)

        def round_rest_by_pairs(name, first):
            for pair in TILE_PAIRS:
                round_weight(name, pair, first, P, "vector")

        def quantise_weight(name, tiles):
            words, scales = weights[name]
            flat = grouped[name][:].rearrange("p t m j -> p (t m j)")
            nc.vector.quantize_mx(
                out=words[:, tiles.start * P : tiles.stop * P].bitcast(FP8X4),
                scales=scales[:, tiles.start * P : tiles.stop * P],
                in_=flat[:, PACK * tiles.start * P : PACK * tiles.stop * P],
            )

        def edges(c):
            return slice(c * CHUNK, (c + 1) * CHUNK)

        def product(bank, terms, c):
            for t in range(PACK):
                places = slice(t * P, (t + 1) * P)
                for n, (name, (words, scales)) in enumerate(terms):
                    w_words, w_scales = weights[name]
                    nc.tensor.matmul_mx(
                        out=bank[:, t, :],
                        lhsT=w_words[:, places].bitcast(FP8X4),
                        lhsT_scale=w_scales[:, places],
                        rhs=words[:, edges(c)].bitcast(FP8X4),
                        rhs_scale=scales[:, edges(c)],
                        start=(n == 0),
                        stop=(n == len(terms) - 1),
                    )

        def add_term(c, name, operand, opens):
            w_words, w_scales = weights[name]
            words, scales = picked[operand]
            for t in range(PACK):
                places = slice(t * P, (t + 1) * P)
                nc.tensor.matmul_mx(
                    out=sums[c][:, t, :],
                    lhsT=w_words[:, places].bitcast(FP8X4),
                    lhsT_scale=w_scales[:, places],
                    rhs=words[:, edges(c)].bitcast(FP8X4),
                    rhs_scale=scales[:, edges(c)],
                    start=(opens and t == 0),
                    stop=(not opens and t == PACK - 1),
                )

        hidden = keep.tile([P, S, PACK], BF16, name="hidden", align_bytes=64)
        h_words = keep.tile([P, S], U32, name="h_words", align_bytes=64)
        h_scales = keep.tile([P, S], U8, name="h_scales", align_bytes=64)
        sums, plain, sloped, scores, values, exps, message = {}, {}, {}, {}, {}, {}, {}

        def open_sums(c, name, operand):
            sums[c] = psum.tile([P, PACK, CHUNK], F32, name=f"y{c}", tag=f"y{c % LAST}")
            add_term(c, name, operand, True)

        def interleaved(c):
            return sums[c][:].rearrange("p t (r n) -> p r n t", r=PACK)

        def slope_chunk(c, dead):
            plain[c] = interleaved(c)
            sloped[c] = dead.rearrange("p r (n t) -> p r n t", t=PACK)
            nc.scalar.activation(sloped[c], interleaved(c), ACT.Copy, scale=SLOPE)

        def slope_last_chunk():
            both = reuse.tile([P, 2, PACK, CHUNK // PACK, PACK], BF16, name="both", offset=0, align_bytes=64)
            plain[LAST], sloped[LAST] = both[:, 0], both[:, 1]
            nc.scalar.copy(plain[LAST], interleaved(LAST))
            nc.scalar.activation(sloped[LAST], interleaved(LAST), ACT.Copy, scale=SLOPE)

        def leaky_chunk(c):
            target = hidden[:, edges(c), :].rearrange("p (r n) t -> p r n t", r=PACK)
            nc.vector.tensor_tensor(target, plain[c], sloped[c], ALU.max)

        def quantise_hidden(c):
            nc.vector.quantize_mx(
                out=h_words[:, edges(c)].bitcast(FP8X4),
                scales=h_scales[:, edges(c)],
                in_=hidden[:, edges(c), :].rearrange("p n t -> p (n t)"),
            )

        out_rows = out_0.rearrange("(p t) n -> p t n", t=PACK)
        out_words = keep.tile([P, S], U32, name="out_words", align_bytes=64)
        out_scales = keep.tile([P, S], U8, name="out_scales", align_bytes=64)
        out_words_dram = out_1[0].rearrange("p c r -> p (c r)").bitcast(I32)
        rounded = keep.tile([P, S, PACK], BF16, name="rounded", align_bytes=64)

        def score_chunk(c):
            scores[c] = psum.tile([P, PACK, CHUNK], F32, name=f"score{c}", tag=f"y{LAST if c == 0 else c % LAST}")
            product(scores[c], (("w3", (h_words, h_scales)),), c)

        def exp_chunk(c):
            exps[c] = keep.tile([P, PACK, CHUNK], F32, name=f"e{c}")
            nc.scalar.activation(exps[c][:], scores[c][:], ACT.Exp)

        def value_chunk(c):
            values[c] = psum.tile([P, PACK, CHUNK], F32, name=f"value{c}", tag=f"v{c}")
            product(values[c], (("w4", picked["src"]),), c)

        def message_chunk(c):
            message[c] = keep.tile([P, PACK, CHUNK], F32, name=f"result{c}")
            cuts = (0, SCALAR_LAST_EDGES, CHUNK) if c == LAST else (0, CHUNK)
            for first, last in zip(cuts, cuts[1:]):
                part = slice(first, last)
                nc.vector.tensor_tensor(message[c][:, :, part], values[c][:, :, part], exps[c][:, :, part], ALU.mult)
            nc.sync.dma_start(out_rows[:, :, edges(c)], message[c][:])

        def round_message(c, engine, first, last):
            target = rounded[:, c * CHUNK + first : c * CHUNK + last, :]
            source = message[c][:, :, first:last]
            if engine == "gpsimd":
                convert(target, source.rearrange("p t n -> p n t"), engine)
            else:
                run = 8 if engine == "scalar" else 4
                target = target.rearrange("p (g i) t -> p g t i", i=run)
                convert(target, source.rearrange("p t (g i) -> p g t i", i=run), engine)

        def quantise_message(first, count):
            cols = slice(first * CHUNK, (first + count) * CHUNK)
            nc.vector.quantize_mx(
                out=out_words[:, cols].bitcast(FP8X4),
                scales=out_scales[:, cols],
                in_=rounded[:, cols, :].rearrange("p n t -> p (n t)"),
            )

        def store_words(first, count):
            cols = slice(first * CHUNK, (first + count) * CHUNK)
            nc.sync.dma_start(out_words_dram[:, cols], out_words[:, cols].bitcast(I32))

        idle = psum.tile([WARM_UP_ROWS, S], F32, name="idle", tag=f"y{LAST}")
        src_words, src_scales = picked["src"]
        for n in range(WARM_UP_PASSES):
            places = slice(n * P, n * P + WARM_UP_ROWS)
            nc.tensor.matmul_mx(
                out=idle[:],
                lhsT=src_words[:, places].bitcast(FP8X4),
                lhsT_scale=src_scales[:, places],
                rhs=src_words[:].bitcast(FP8X4),
                rhs_scale=src_scales[:],
                start=True,
                stop=True,
            )

        round_weight("w1", ALL_TILES, 0, P, "scalar")
        quantise_weight("w1", ALL_TILES)
        for c in range(2):
            open_sums(c, "w1", "src")
        round_weight("w2", ALL_TILES, 0, SCALAR_W2, "scalar")
        round_rest_by_pairs("w2", SCALAR_W2)
        for pair in TILE_PAIRS:
            quantise_weight("w2", pair)
        round_weight("w4", ALL_TILES, 0, SCALAR_W4, "scalar")
        round_rest_by_pairs("w4", SCALAR_W4)
        for pair in TILE_PAIRS:
            quantise_weight("w4", pair)
        for c in range(2):
            add_term(c, "w2", "dst", False)
        open_sums(2, "w2", "dst")
        add_term(2, "w1", "src", False)
        for c in range(2):
            value_chunk(c)

        for c in range(2):
            slope_chunk(c, raw["w4"][:, :, edges(c)])
            leaky_chunk(c)
        open_sums(LAST, "w2", "dst")
        add_term(LAST, "w1", "src", False)
        for c in range(2, CHUNKS):
            value_chunk(c)
        round_weight("w3", ALL_TILES, 0, SCALAR_W3_FIRST, "scalar")
        round_weight("w3", ALL_TILES, SCALAR_W3_FIRST, SCALAR_W3, "scalar")
        round_weight("w3", ALL_TILES, SCALAR_W3, SCALAR_W3 + GPSIMD_W3, "gpsimd")
        round_rest_by_pairs("w3", SCALAR_W3 + GPSIMD_W3)
        quantise_hidden(0)
        for pair in TILE_PAIRS:
            quantise_weight("w3", pair)
        score_chunk(0)
        slope_chunk(2, raw["w3"][:, :, 0:CHUNK])
        slope_last_chunk()
        leaky_chunk(2)
        for c in (1, 2):
            quantise_hidden(c)
            score_chunk(c)
        leaky_chunk(LAST)
        quantise_hidden(LAST)
        score_chunk(LAST)

        for c in range(CHUNKS):
            exp_chunk(c)
            message_chunk(c)
        round_message(0, "gpsimd", 0, CHUNK)
        round_message(1, "scalar", 0, CHUNK)
        round_message(2, "scalar", 0, CHUNK)
        quantise_message(0, 2)
        store_words(0, 2)
        round_message(LAST, "vector", SCALAR_LAST_EDGES, CHUNK)
        round_message(LAST, "scalar", 0, SCALAR_LAST_EDGES)
        quantise_message(2, 1)
        quantise_message(LAST, 1)
        store_words(2, 2)

        for q in range(QUADRANTS):
            queue = nc.scalar if q % 2 else nc.sync
            queue.dma_start(
                out_2[0][4 * q : 4 * q + 4, :].bitcast(I32),
                out_scales[32 * q : 32 * q + 4, :].bitcast(I32),
            )
